import numpy as np
import ml_dtypes


def mxq(x, axis, fmt="e4m3"):
    dtype, down = {"e4m3": (ml_dtypes.float8_e4m3fn, 7), "e5m2": (ml_dtypes.float8_e5m2, 14)}[fmt]
    v = np.moveaxis(np.asarray(x, np.float32).astype(ml_dtypes.bfloat16).astype(np.float64), axis, -1)
    blocks = v.reshape(v.shape[:-1] + (-1, 32))
    amax = np.abs(blocks).max(-1, keepdims=True)
    byte = np.maximum(np.where(amax > 0, np.frexp(amax)[1] - 1 + 127, 0) - down, 1)
    scale = np.exp2(byte - 127.0)
    codes = (blocks / scale).astype(np.float32).astype(dtype).astype(np.float64)
    return np.moveaxis((codes * scale).reshape(v.shape), -1, axis)


WIDE = False


def mx_kscale(k):
    if not WIDE:
        return np.ones(k)
    levels = np.array([10, -10, 5, -5, 0])
    if k % 512:
        return np.exp2(np.random.permutation(np.resize(levels, k // 32))).repeat(32)
    a = np.empty((k // 512, 16))
    for p in range(k // 512):
        a[p, :8] = np.random.permutation(np.resize(levels, 8))
        for g in range(8):
            far = levels[np.abs(levels - a[p, g]) >= 10]
            a[p, g + 8] = far[np.random.randint(len(far))]
    return np.exp2(a.ravel()).repeat(32)


def f64(x):
    return np.asarray(x).astype(np.float64)


def striped(idx):
    return np.tile(idx.reshape(-1, 16).T, (8, 1)).astype(np.uint16)


def unstriped(offs):
    return offs[:16].T.reshape(-1).astype(np.int64)


E2M1 = np.array([0.0, 0.5, 1.0, 1.5, 2.0, 3.0, 4.0, 6.0, -0.0, -0.5, -1.0, -1.5, -2.0, -3.0, -4.0, -6.0])


def pack_fp4(w):
    k, n = w.shape
    w = f64(np.asarray(w, np.float32).astype(ml_dtypes.bfloat16)).reshape(k // 32, 32, n)
    amax = np.abs(w).max(1)
    mant, ex = np.frexp(amax / 6.0)
    byte = np.clip(np.where(amax > 0, np.where(mant > 0.5, ex, ex - 1) + 127, 1), 1, 254)
    scaled = (w * np.exp2(127.0 - byte)[:, None, :]).reshape(k, n).astype(np.float32)
    c = np.ascontiguousarray(scaled.reshape(k // 512, 128, 4, n).transpose(0, 1, 3, 2)).astype(ml_dtypes.float4_e2m1fn).view(np.uint8) & 0xF
    words = (c[..., 0::2] | (c[..., 1::2] << 4)).reshape(k // 512, 128, 2 * n)
    return np.ascontiguousarray(words), np.ascontiguousarray(byte.astype(np.uint8).reshape(k // 512, 16, n))


def unpack_fp4(words, scales):
    g, _, n = scales.shape
    words = np.ascontiguousarray(words).reshape(g, 128, n, 2)
    nib = np.empty((g, 128, n, 4), np.uint8)
    nib[..., 0::2] = words & 0xF
    nib[..., 1::2] = words >> 4
    vals = E2M1[nib] * np.repeat(np.exp2(scales.astype(np.float64) - 127.0), 8, axis=1)[..., None]
    return vals.transpose(0, 1, 3, 2).reshape(g * 512, n)


def relu(v):
    return np.maximum(v, 0.0)


K, T, S, N = 1024, 1024, 512, 256
P = 2 ** 7


def setup_inputs():
    n = np.random.standard_normal
    s = mx_kscale(K)[:, None]
    packed_w1 = pack_fp4(n((K, N)) / np.sqrt(K) / s)
    return {
        "xT": (n((K, T)) * s).astype(np.float32),
        "gate": np.tile(np.random.uniform(0.2, 1.0, S), (P, 1)).astype(np.float32),
        "res": n((N, T)).astype(np.float32),
        "w1_words": packed_w1[0],
        "w1_scales": packed_w1[1],
        "offs": striped(np.random.permutation(T)[:S]),
    }


def reference(xT, gate, res, w1_words, w1_scales, offs):
    r = f64(res)[:, unstriped(offs)]
    xq = mxq(f64(xT)[:, unstriped(offs)], 0, "e4m3")
    y = relu(unpack_fp4(w1_words, w1_scales).T @ xq)
    out = f64(res).copy()
    out[:, unstriped(offs)] = r + y * f64(gate)[:1]
    return out

@@ -1,0 +1,128 @@
+from contextlib import ExitStack
+
+import concourse.mybir as mybir
+
+K, T, S, N = 1024, 1024, 512, 256
+FLOPS = 2 * K * S * N
+
+F32 = mybir.dt.float32
+BF16 = mybir.dt.bfloat16
+U32 = mybir.dt.uint32
+I32 = mybir.dt.int32
+U16 = mybir.dt.uint16
+U8 = mybir.dt.uint8
+FP8X4 = mybir.dt.float8_e4m3fn_x4
+FP4X4 = mybir.dt.float4_e2m1fn_x4
+ALU = mybir.AluOpType
+
+P = 128
+PASSES = 2
+BLOCKS = 2
+HALF = S // 2
+
+CHUNKS = [
+    [(0, 512, 512), (512, 1024, 160)],
+    [(0, 512, 512), (512, 1024, 160)],
+    [(0, 512, 512), (512, 1024, 320)],
+    [(0, 512, 512), (512, 1024, 160)],
+]
+
+
+def tile_picked_modres_linrelu_l_kernel(tc, xT, gate, res, w1_words, w1_scales, offs, out):
+    nc = tc.nc
+    with ExitStack() as ctx:
+        keep = ctx.enter_context(tc.tile_pool(name="keep", bufs=1))
+        psum = ctx.enter_context(tc.psum_pool(name="psum", bufs=1))
+
+        offsets = keep.tile([P, S // 16], U16, name="offsets")
+        x_rows = xT.rearrange("(z p u e) t -> z u p e t", z=PASSES, p=P, u=2, e=2)
+
+        w_scales = keep.tile([P, PASSES * N], U8, name="w_scales", align_bytes=64)
+        nc.gpsimd.memset(w_scales[:].bitcast(I32), 0)
+
+        raws = []
+        for i in range(4):
+            row = []
+            for c, (c0, c1, unused) in enumerate(CHUNKS[i]):
+                raw = keep.tile([P, 2, c1 - c0], F32, name=f"raw{i}_{c}")
+                nc.sync.dma_start(out=raw[:], in_=x_rows[i // 2, i % 2][:, :, c0:c1])
+                row.append(raw)
+                if i == 0 and c == 0:
+                    nc.sync.dma_start(offsets[:], offs)
+            raws.append(row)
+
+        windows = [keep.tile([P, T], F32, name=f"res{b}") for b in range(BLOCKS)]
+        nc.sync.dma_start(out=windows[0][:], in_=res[0:P, :])
+        w_words = keep.tile([P, PASSES, 2 * N], U8, name="w_words", align_bytes=64)
+        nc.sync.dma_start(out=w_words[:].bitcast(I32), in_=w1_words.rearrange("z p c -> p z c").bitcast(I32))
+        for q in range(4):
+            nc.sync.dma_start(
+                out=w_scales[32 * q : 32 * q + 4, :].rearrange("r (z c) -> r z c", z=PASSES).bitcast(I32),
+                in_=w1_scales[:, 4 * q : 4 * q + 4, :].rearrange("z r c -> r z c").bitcast(I32),
+            )
+        nc.sync.dma_start(out=windows[1][:], in_=res[P : 2 * P, :])
+        gates = keep.tile([P, S], F32, name="gates")
+        nc.sync.dma_start(out=gates[:], in_=gate)
+
+        codes = [keep.tile([P, S], U32, name=f"codes{z}", align_bytes=64) for z in range(PASSES)]
+        scales = [keep.tile([P, S], U8, name=f"scales{z}", align_bytes=64) for z in range(PASSES)]
+
+        def cast(i):
+            pairs = keep.tile([P, T], U32, name=f"pairs{i}", tag=f"pairs{i}")
+            view = pairs[:].bitcast(BF16).rearrange("p (t e) -> p t e", e=2)
+            for raw, (c0, c1, share) in zip(raws[i], CHUNKS[i]):
+                src = raw[:].rearrange("p e t -> p t e")
+                nc.scalar.copy(out=view[:, c0 : c0 + share, :], in_=src[:, 0:share, :])
+                if c0 + share < c1:
+                    nc.vector.tensor_copy(out=view[:, c0 + share : c1, :], in_=src[:, share:, :])
+            return pairs
+
+        quads0 = keep.tile([P, S, 2], U32, name="quads0", align_bytes=64)
+        for u in range(2):
+            pairs = cast(u)
+            nc.vector.tensor_copy(quads0[:, :, u], pairs[:].indirect(offsets[:]))
+        nc.vector.quantize_mx(
+            out=codes[0][:].bitcast(FP8X4), scales=scales[0][:],
+            in_=quads0[:].rearrange("p s u -> p (s u)").bitcast(BF16),
+        )
+
+        picked1 = [keep.tile([P, 2, HALF], U32, name=f"picked1_{h}") for h in range(2)]
+        quads1 = [keep.tile([P, HALF, 2], U32, name=f"quads1_{h}", tag=f"quads1_{h}", align_bytes=64) for h in range(2)]
+        for u in range(2):
+            pairs = cast(2 + u)
+            for h in range(2):
+                nc.vector.tensor_copy(picked1[h][:, u, :], pairs[:].indirect(offsets[:, 16 * h : 16 * h + 16]))
+        for h in range(2):
+            nc.scalar.copy(out=quads1[h][:], in_=picked1[h][:].rearrange("p u s -> p s u"))
+
+        olds = [keep.tile([P, S], F32, name="old0", tag="pairs3")]
+        nc.vector.tensor_copy(olds[0][:], windows[0][:].indirect(offsets[:]))
+        for h in range(2):
+            cols = slice(h * HALF, (h + 1) * HALF)
+            nc.vector.quantize_mx(
+                out=codes[1][:, cols].bitcast(FP8X4), scales=scales[1][:, cols],
+                in_=quads1[h][:].rearrange("p s u -> p (s u)").bitcast(BF16),
+            )
+        olds.append(keep.tile([P, S], F32, name="old1", tag="quads1_1", align_bytes=64))
+        nc.vector.tensor_copy(olds[1][:], windows[1][:].indirect(offsets[:]))
+
+        accs = [psum.tile([P, S], F32, name=f"acc{b}") for b in range(BLOCKS)]
+        for z in range(PASSES):
+            for b in range(BLOCKS):
+                nc.tensor.matmul_mx(
+                    out=accs[b][:],
+                    lhsT=w_words[:, z, 2 * P * b : 2 * P * (b + 1)].bitcast(FP4X4),
+                    lhsT_scale=w_scales[:, z * N + P * b : z * N + P * (b + 1)],
+                    rhs=codes[z][:].bitcast(FP8X4),
+                    rhs_scale=scales[z][:],
+                    start=(z == 0),
+                    stop=(z == PASSES - 1),
+                )
+
+        for b in range(BLOCKS):
+            gated = keep.tile([P, S], F32, name=f"gated{b}")
+            nc.vector.scalar_tensor_tensor(
+                out=gated[:], in0=accs[b][:], scalar=0.0, in1=gates[:], op0=ALU.max, op1=ALU.mult
+            )
+            nc.vector.tensor_tensor(windows[b][:].indirect(offsets[:]), olds[b][:], gated[:], ALU.add)
+            nc.sync.dma_start(out=out[P * b : P * (b + 1), :], in_=windows[b][:])

@@ -1,6 +1,7 @@
 from contextlib import ExitStack
 
 import concourse.mybir as mybir
+from concourse.masks import make_identity
 
 K, T, S, N = 1024, 1024, 512, 256
 FLOPS = 2 * K * S * N
@@ -14,6 +15,7 @@ U8 = mybir.dt.uint8
 FP8X4 = mybir.dt.float8_e4m3fn_x4
 FP4X4 = mybir.dt.float4_e2m1fn_x4
 ALU = mybir.AluOpType
+ACT = mybir.ActivationFunctionType
 
 P = 128
 PASSES = 2
@@ -21,9 +23,9 @@ BLOCKS = 2
 HALF = S // 2
 
 CHUNKS = [
+    [(0, 1024, 352)],
     [(0, 512, 512), (512, 1024, 160)],
-    [(0, 512, 512), (512, 1024, 160)],
-    [(0, 512, 512), (512, 1024, 320)],
+    [(0, 512, 512), (512, 1024, 384)],
     [(0, 512, 512), (512, 1024, 160)],
 ]
 
@@ -44,7 +46,7 @@ def tile_picked_modres_linrelu_l_kernel(tc, xT, gate, res, w1_words, w1_scales, 
         for i in range(4):
             row = []
             for c, (c0, c1, unused) in enumerate(CHUNKS[i]):
-                raw = keep.tile([P, 2, c1 - c0], F32, name=f"raw{i}_{c}")
+                raw = keep.tile([P, 2, c1 - c0], F32, name=f"raw{i}_{c}", tag=f"raw{i}_{c}", align_bytes=64)
                 nc.sync.dma_start(out=raw[:], in_=x_rows[i // 2, i % 2][:, :, c0:c1])
                 row.append(raw)
                 if i == 0 and c == 0:
@@ -61,10 +63,15 @@ def tile_picked_modres_linrelu_l_kernel(tc, xT, gate, res, w1_words, w1_scales, 
                 in_=w1_scales[:, 4 * q : 4 * q + 4, :].rearrange("z r c -> r z c").bitcast(I32),
             )
         nc.sync.dma_start(out=windows[1][:], in_=res[P : 2 * P, :])
-        gates = keep.tile([P, S], F32, name="gates")
-        nc.sync.dma_start(out=gates[:], in_=gate)
+        gate_rows = keep.tile([P, S], F32, name="gate_rows")
+        nc.sync.dma_start(out=gate_rows[:], in_=gate)
+        gates = keep.tile([P, S // P], F32, name="gates")
+        with nc.allow_non_contiguous_dma(reason="one gate value a partition"):
+            nc.sync.dma_start(out=gates[:], in_=gate[0, :].rearrange("(c p) -> p c", p=P))
 
-        codes = [keep.tile([P, S], U32, name=f"codes{z}", align_bytes=64) for z in range(PASSES)]
+        identity = keep.tile([P, P], F32, name="identity")
+        make_identity(nc, identity[:])
+
         scales = [keep.tile([P, S], U8, name=f"scales{z}", align_bytes=64) for z in range(PASSES)]
 
         def cast(i):
@@ -81,48 +88,70 @@ def tile_picked_modres_linrelu_l_kernel(tc, xT, gate, res, w1_words, w1_scales, 
         for u in range(2):
             pairs = cast(u)
             nc.vector.tensor_copy(quads0[:, :, u], pairs[:].indirect(offsets[:]))
+        pairs_c = cast(2)
+        codes = [
+            keep.tile([P, S], U32, name="codes0", tag="raw2_0", align_bytes=64),
+            keep.tile([P, S], U32, name="codes1", align_bytes=64),
+        ]
         nc.vector.quantize_mx(
             out=codes[0][:].bitcast(FP8X4), scales=scales[0][:],
             in_=quads0[:].rearrange("p s u -> p (s u)").bitcast(BF16),
         )
 
         picked1 = [keep.tile([P, 2, HALF], U32, name=f"picked1_{h}") for h in range(2)]
-        quads1 = [keep.tile([P, HALF, 2], U32, name=f"quads1_{h}", tag=f"quads1_{h}", align_bytes=64) for h in range(2)]
+        quads1 = keep.tile([P, S, 2], U32, name="quads1", align_bytes=64)
         for u in range(2):
-            pairs = cast(2 + u)
+            pairs = pairs_c if u == 0 else cast(3)
             for h in range(2):
                 nc.vector.tensor_copy(picked1[h][:, u, :], pairs[:].indirect(offsets[:, 16 * h : 16 * h + 16]))
         for h in range(2):
-            nc.scalar.copy(out=quads1[h][:], in_=picked1[h][:].rearrange("p u s -> p s u"))
+            nc.scalar.copy(out=quads1[:, HALF * h : HALF * (h + 1), :], in_=picked1[h][:].rearrange("p u s -> p s u"))
 
-        olds = [keep.tile([P, S], F32, name="old0", tag="pairs3")]
+        olds = [keep.tile([P, S], F32, name=f"old{b}") for b in range(BLOCKS)]
         nc.vector.tensor_copy(olds[0][:], windows[0][:].indirect(offsets[:]))
-        for h in range(2):
-            cols = slice(h * HALF, (h + 1) * HALF)
-            nc.vector.quantize_mx(
-                out=codes[1][:, cols].bitcast(FP8X4), scales=scales[1][:, cols],
-                in_=quads1[h][:].rearrange("p s u -> p (s u)").bitcast(BF16),
-            )
-        olds.append(keep.tile([P, S], F32, name="old1", tag="quads1_1", align_bytes=64))
+        nc.vector.quantize_mx(
+            out=codes[1][:].bitcast(FP8X4), scales=scales[1][:],
+            in_=quads1[:].rearrange("p s u -> p (s u)").bitcast(BF16),
+        )
         nc.vector.tensor_copy(olds[1][:], windows[1][:].indirect(offsets[:]))
 
-        accs = [psum.tile([P, S], F32, name=f"acc{b}") for b in range(BLOCKS)]
+        def weights(z, b):
+            return (
+                w_words[:, z, 2 * P * b : 2 * P * (b + 1)].bitcast(FP4X4),
+                w_scales[:, z * N + P * b : z * N + P * (b + 1)],
+            )
+
+        acc0 = psum.tile([P, S], F32, name="acc0")
+        accs = [psum.tile([P, P], F32, name=f"acc1_{c}") for c in range(4)]
         for z in range(PASSES):
-            for b in range(BLOCKS):
+            w, ws = weights(z, 0)
+            nc.tensor.matmul_mx(
+                out=acc0[:], lhsT=w, lhsT_scale=ws, rhs=codes[z][:].bitcast(FP8X4), rhs_scale=scales[z][:],
+                start=(z == 0), stop=(z == PASSES - 1),
+            )
+            w, ws = weights(z, 1)
+            for c in range(4):
+                toks = slice(P * c, P * (c + 1))
                 nc.tensor.matmul_mx(
-                    out=accs[b][:],
-                    lhsT=w_words[:, z, 2 * P * b : 2 * P * (b + 1)].bitcast(FP4X4),
-                    lhsT_scale=w_scales[:, z * N + P * b : z * N + P * (b + 1)],
-                    rhs=codes[z][:].bitcast(FP8X4),
-                    rhs_scale=scales[z][:],
-                    start=(z == 0),
-                    stop=(z == PASSES - 1),
+                    out=accs[c][:], lhsT=codes[z][:, toks].bitcast(FP8X4), lhsT_scale=scales[z][:, toks],
+                    rhs=w, rhs_scale=ws, start=(z == 0), stop=(z == PASSES - 1),
                 )
 
+        gated = [keep.tile([P, S], F32, name=f"gated{b}") for b in range(BLOCKS)]
+        nc.vector.scalar_tensor_tensor(
+            out=gated[0][:], in0=acc0[:], scalar=0.0, in1=gate_rows[:], op0=ALU.max, op1=ALU.mult
+        )
+        for h in range(2):
+            turned = psum.tile([P, 2, P], F32, name=f"turned{h}")
+            for c in range(2):
+                active = keep.tile([P, P], F32, name=f"active{h}{c}")
+                nc.scalar.activation(out=active[:], in_=accs[2 * h + c][:], func=ACT.Relu)
+                scaled = keep.tile([P, P], F32, name=f"scaled{h}{c}")
+                nc.scalar.activation(
+                    out=scaled[:], in_=active[:], func=ACT.Copy, scale=gates[:, 2 * h + c : 2 * h + c + 1]
+                )
+                nc.tensor.transpose(turned[:, c, :], scaled[:], identity[:])
+            nc.scalar.copy(out=gated[1][:, HALF * h : HALF * (h + 1)], in_=turned[:].rearrange("p c t -> p (c t)"))
         for b in range(BLOCKS):
-            gated = keep.tile([P, S], F32, name=f"gated{b}")
-            nc.vector.scalar_tensor_tensor(
-                out=gated[:], in0=accs[b][:], scalar=0.0, in1=gates[:], op0=ALU.max, op1=ALU.mult
-            )
-            nc.vector.tensor_tensor(windows[b][:].indirect(offsets[:]), olds[b][:], gated[:], ALU.add)
+            nc.vector.tensor_tensor(windows[b][:].indirect(offsets[:]), olds[b][:], gated[b][:], ALU.add)
             nc.sync.dma_start(out=out[P * b : P * (b + 1), :], in_=windows[b][:])

@@ -41,6 +41,11 @@ def tile_picked_modres_linrelu_l_kernel(tc, xT, gate, res, w1_words, w1_scales, 
 
         w_scales = keep.tile([P, PASSES * N], U8, name="w_scales", align_bytes=64)
         nc.gpsimd.memset(w_scales[:].bitcast(I32), 0)
+        for q in range(4):
+            nc.gpsimd.dma_start(
+                out=w_scales[32 * q : 32 * q + 4, :].rearrange("r (z c) -> r z c", z=PASSES).bitcast(I32),
+                in_=w1_scales[:, 4 * q : 4 * q + 4, :].rearrange("z r c -> r z c").bitcast(I32),
+            )
 
         raws = []
         for i in range(4):
@@ -57,11 +62,6 @@ def tile_picked_modres_linrelu_l_kernel(tc, xT, gate, res, w1_words, w1_scales, 
         nc.sync.dma_start(out=windows[0][:], in_=res[0:P, :])
         w_words = keep.tile([P, PASSES, 2 * N], U8, name="w_words", align_bytes=64)
         nc.sync.dma_start(out=w_words[:].bitcast(I32), in_=w1_words.rearrange("z p c -> p z c").bitcast(I32))
-        for q in range(4):
-            nc.sync.dma_start(
-                out=w_scales[32 * q : 32 * q + 4, :].rearrange("r (z c) -> r z c", z=PASSES).bitcast(I32),
-                in_=w1_scales[:, 4 * q : 4 * q + 4, :].rearrange("z r c -> r z c").bitcast(I32),
-            )
         nc.sync.dma_start(out=windows[1][:], in_=res[P : 2 * P, :])
         gate_rows = keep.tile([P, S], F32, name="gate_rows")
         nc.sync.dma_start(out=gate_rows[:], in_=gate)

@@ -23,8 +23,8 @@ BLOCKS = 2
 HALF = S // 2
 
 CHUNKS = [
-    [(0, 1024, 352)],
-    [(0, 512, 512), (512, 1024, 160)],
+    [(0, 512, 512), (512, 1024, 192)],
+    [(0, 512, 512), (512, 1024, 224)],
     [(0, 512, 512), (512, 1024, 384)],
     [(0, 512, 512), (512, 1024, 160)],
 ]

@@ -23,10 +23,10 @@ BLOCKS = 2
 HALF = S // 2
 
 CHUNKS = [
+    [(0, 512, 512), (512, 1024, 256)],
+    [(0, 512, 512), (512, 1024, 320)],
+    [(0, 512, 512), (512, 1024, 256)],
     [(0, 512, 512), (512, 1024, 192)],
-    [(0, 512, 512), (512, 1024, 224)],
-    [(0, 512, 512), (512, 1024, 384)],
-    [(0, 512, 512), (512, 1024, 160)],
 ]
 
 
@@ -41,11 +41,17 @@ def tile_picked_modres_linrelu_l_kernel(tc, xT, gate, res, w1_words, w1_scales, 
 
         w_scales = keep.tile([P, PASSES * N], U8, name="w_scales", align_bytes=64)
         nc.gpsimd.memset(w_scales[:].bitcast(I32), 0)
+        gate_chunks = keep.tile([P, P], F32, name="gate_chunks")
+        nc.gpsimd.memset(gate_chunks[:], 0.0)
+        nc.gpsimd.dma_start(out=gate_chunks[0 : S // P, :], in_=gate[0, :].rearrange("(c p) -> c p", p=P))
         for q in range(4):
-            nc.gpsimd.dma_start(
+            queue = nc.scalar if q < 2 else nc.gpsimd
+            queue.dma_start(
                 out=w_scales[32 * q : 32 * q + 4, :].rearrange("r (z c) -> r z c", z=PASSES).bitcast(I32),
                 in_=w1_scales[:, 4 * q : 4 * q + 4, :].rearrange("z r c -> r z c").bitcast(I32),
             )
+        identity = keep.tile([P, P], F32, name="identity")
+        make_identity(nc, identity[:])
 
         raws = []
         for i in range(4):
@@ -58,100 +64,141 @@ def tile_picked_modres_linrelu_l_kernel(tc, xT, gate, res, w1_words, w1_scales, 
                     nc.sync.dma_start(offsets[:], offs)
             raws.append(row)
 
+        w_words = [keep.tile([P, 2 * N], U8, name=f"w_words{z}", align_bytes=64) for z in range(PASSES)]
         windows = [keep.tile([P, T], F32, name=f"res{b}") for b in range(BLOCKS)]
-        nc.sync.dma_start(out=windows[0][:], in_=res[0:P, :])
-        w_words = keep.tile([P, PASSES, 2 * N], U8, name="w_words", align_bytes=64)
-        nc.sync.dma_start(out=w_words[:].bitcast(I32), in_=w1_words.rearrange("z p c -> p z c").bitcast(I32))
         nc.sync.dma_start(out=windows[1][:], in_=res[P : 2 * P, :])
-        gate_rows = keep.tile([P, S], F32, name="gate_rows")
-        nc.sync.dma_start(out=gate_rows[:], in_=gate)
-        gates = keep.tile([P, S // P], F32, name="gates")
-        with nc.allow_non_contiguous_dma(reason="one gate value a partition"):
-            nc.sync.dma_start(out=gates[:], in_=gate[0, :].rearrange("(c p) -> p c", p=P))
+        nc.sync.dma_start(out=w_words[0][:].bitcast(I32), in_=w1_words[0].bitcast(I32))
+        nc.sync.dma_start(out=windows[0][:], in_=res[0:P, :])
+        gate_rows = keep.tile([P, HALF], F32, name="gate_rows")
+        nc.sync.dma_start(out=gate_rows[:], in_=gate[:, 0:HALF])
+        nc.sync.dma_start(out=w_words[1][:].bitcast(I32), in_=w1_words[1].bitcast(I32))
 
-        identity = keep.tile([P, P], F32, name="identity")
-        make_identity(nc, identity[:])
-
-        scales = [keep.tile([P, S], U8, name=f"scales{z}", align_bytes=64) for z in range(PASSES)]
+        gates_turned = psum.tile([P, P], F32, name="gates_turned", tag="turned01")
+        nc.tensor.transpose(gates_turned[:], gate_chunks[:], identity[:])
 
         def cast(i):
             pairs = keep.tile([P, T], U32, name=f"pairs{i}", tag=f"pairs{i}")
             view = pairs[:].bitcast(BF16).rearrange("p (t e) -> p t e", e=2)
             for raw, (c0, c1, share) in zip(raws[i], CHUNKS[i]):
                 src = raw[:].rearrange("p e t -> p t e")
-                nc.scalar.copy(out=view[:, c0 : c0 + share, :], in_=src[:, 0:share, :])
+                if share > 0:
+                    nc.scalar.copy(out=view[:, c0 : c0 + share, :], in_=src[:, 0:share, :])
                 if c0 + share < c1:
                     nc.vector.tensor_copy(out=view[:, c0 + share : c1, :], in_=src[:, share:, :])
             return pairs
+
+        def half_list(h):
+            return offsets[:, 16 * h : 16 * h + 16]
 
         quads0 = keep.tile([P, S, 2], U32, name="quads0", align_bytes=64)
         for u in range(2):
             pairs = cast(u)
             nc.vector.tensor_copy(quads0[:, :, u], pairs[:].indirect(offsets[:]))
-        pairs_c = cast(2)
-        codes = [
-            keep.tile([P, S], U32, name="codes0", tag="raw2_0", align_bytes=64),
-            keep.tile([P, S], U32, name="codes1", align_bytes=64),
+
+        codes0, scales0 = [], []
+        picked1 = [
+            keep.tile([P, 2, HALF], U32, name=f"picked1_{h}", tag=f"picked1_{h}", align_bytes=64) for h in range(2)
         ]
-        nc.vector.quantize_mx(
-            out=codes[0][:].bitcast(FP8X4), scales=scales[0][:],
-            in_=quads0[:].rearrange("p s u -> p (s u)").bitcast(BF16),
-        )
-
-        picked1 = [keep.tile([P, 2, HALF], U32, name=f"picked1_{h}") for h in range(2)]
-        quads1 = keep.tile([P, S, 2], U32, name="quads1", align_bytes=64)
         for u in range(2):
-            pairs = pairs_c if u == 0 else cast(3)
-            for h in range(2):
-                nc.vector.tensor_copy(picked1[h][:, u, :], pairs[:].indirect(offsets[:, 16 * h : 16 * h + 16]))
-        for h in range(2):
-            nc.scalar.copy(out=quads1[:, HALF * h : HALF * (h + 1), :], in_=picked1[h][:].rearrange("p u s -> p s u"))
-
-        olds = [keep.tile([P, S], F32, name=f"old{b}") for b in range(BLOCKS)]
-        nc.vector.tensor_copy(olds[0][:], windows[0][:].indirect(offsets[:]))
-        nc.vector.quantize_mx(
-            out=codes[1][:].bitcast(FP8X4), scales=scales[1][:],
-            in_=quads1[:].rearrange("p s u -> p (s u)").bitcast(BF16),
-        )
-        nc.vector.tensor_copy(olds[1][:], windows[1][:].indirect(offsets[:]))
-
-        def weights(z, b):
-            return (
-                w_words[:, z, 2 * P * b : 2 * P * (b + 1)].bitcast(FP4X4),
-                w_scales[:, z * N + P * b : z * N + P * (b + 1)],
+            pairs = cast(2 + u)
+            codes0.append(keep.tile([P, HALF], U32, name=f"codes0_{u}", tag=f"raw{2 + u}_0", align_bytes=64))
+            scales0.append(keep.tile([P, HALF], U8, name=f"scales0_{u}", tag=f"scales0_{u}", align_bytes=64))
+            nc.vector.quantize_mx(
+                out=codes0[u][:].bitcast(FP8X4), scales=scales0[u][:],
+                in_=quads0[:, HALF * u : HALF * (u + 1), :].rearrange("p s u -> p (s u)").bitcast(BF16),
             )
+            for h in range(2):
+                nc.vector.tensor_copy(picked1[h][:, u, :], pairs[:].indirect(half_list(h)))
+        quads1 = [keep.tile([P, HALF, 2], U32, name=f"quads1_{h}", align_bytes=64) for h in range(2)]
+        for h in range(2):
+            nc.scalar.copy(out=quads1[h][:], in_=picked1[h][:].rearrange("p u s -> p s u"))
+        gates = keep.tile([P, S // P], F32, name="gates", tag="picked1_1", align_bytes=64)
+        nc.scalar.copy(out=gates[:], in_=gates_turned[:, 0 : S // P])
 
-        acc0 = psum.tile([P, S], F32, name="acc0")
-        accs = [psum.tile([P, P], F32, name=f"acc1_{c}") for c in range(4)]
-        for z in range(PASSES):
-            w, ws = weights(z, 0)
+        codes1 = [keep.tile([P, HALF], U32, name=f"codes1_{h}", tag=f"codes1_{h}", align_bytes=64) for h in range(2)]
+        scales1 = [keep.tile([P, HALF], U8, name=f"scales1_{h}", align_bytes=64) for h in range(2)]
+        old0 = keep.tile([P, S], F32, name="old0")
+        olds = {(0, 0): old0[:, 0:HALF], (1, 0): old0[:, HALF:S]}
+
+        def pick_old1(h, tag):
+            old = keep.tile([P, HALF], F32, name=f"old1_{h}", tag=tag, align_bytes=64)
+            nc.vector.tensor_copy(old[:], windows[1][:].indirect(half_list(h)))
+            olds[(h, 1)] = old[:]
+
+        pick_old1(0, "old1_0")
+        for h in range(2):
+            nc.vector.quantize_mx(
+                out=codes1[h][:].bitcast(FP8X4), scales=scales1[h][:],
+                in_=quads1[h][:].rearrange("p s u -> p (s u)").bitcast(BF16),
+            )
+        nc.vector.tensor_copy(old0[:], windows[0][:].indirect(offsets[:]))
+
+        def product(acc, z, c, b):
+            toks = slice(P * (c % 2), P * (c % 2 + 1))
+            codes, scales = [codes0, codes1][z][c // 2][:, toks], [scales0, scales1][z][c // 2][:, toks]
             nc.tensor.matmul_mx(
-                out=acc0[:], lhsT=w, lhsT_scale=ws, rhs=codes[z][:].bitcast(FP8X4), rhs_scale=scales[z][:],
+                out=acc, lhsT=codes.bitcast(FP8X4), lhsT_scale=scales,
+                rhs=w_words[z][:, 2 * P * b : 2 * P * (b + 1)].bitcast(FP4X4),
+                rhs_scale=w_scales[:, z * N + P * b : z * N + P * (b + 1)],
                 start=(z == 0), stop=(z == PASSES - 1),
             )
-            w, ws = weights(z, 1)
-            for c in range(4):
-                toks = slice(P * c, P * (c + 1))
-                nc.tensor.matmul_mx(
-                    out=accs[c][:], lhsT=codes[z][:, toks].bitcast(FP8X4), lhsT_scale=scales[z][:, toks],
-                    rhs=w, rhs_scale=ws, start=(z == 0), stop=(z == PASSES - 1),
-                )
 
-        gated = [keep.tile([P, S], F32, name=f"gated{b}") for b in range(BLOCKS)]
-        nc.vector.scalar_tensor_tensor(
-            out=gated[0][:], in0=acc0[:], scalar=0.0, in1=gate_rows[:], op0=ALU.max, op1=ALU.mult
-        )
-        for h in range(2):
-            turned = psum.tile([P, 2, P], F32, name=f"turned{h}")
-            for c in range(2):
-                active = keep.tile([P, P], F32, name=f"active{h}{c}")
-                nc.scalar.activation(out=active[:], in_=accs[2 * h + c][:], func=ACT.Relu)
-                scaled = keep.tile([P, P], F32, name=f"scaled{h}{c}")
-                nc.scalar.activation(
-                    out=scaled[:], in_=active[:], func=ACT.Copy, scale=gates[:, 2 * h + c : 2 * h + c + 1]
+        def scatter(gated, h, b):
+            nc.vector.tensor_tensor(
+                windows[b][:].indirect(half_list(h)), olds[(h, b)], gated[:], ALU.add
+            )
+
+        def gate_on_scalar(sums, h, b, bank):
+            turned = psum.tile([P, 2, P], F32, name=f"turned{h}{b}", tag=bank)
+            c = 0
+            for acc in sums:
+                active = keep.tile([P, acc.shape[1], P], F32, name=f"active{h}{b}{c}")
+                nc.scalar.activation(out=active[:], in_=acc, func=ACT.Relu)
+                for j in range(acc.shape[1]):
+                    scaled = keep.tile([P, P], F32, name=f"scaled{h}{b}{c}")
+                    nc.scalar.activation(
+                        out=scaled[:], in_=active[:, j, :], func=ACT.Copy, scale=gates[:, 2 * h + c : 2 * h + c + 1]
+                    )
+                    nc.tensor.transpose(turned[:, c, :], scaled[:], identity[:])
+                    c = c + 1
+            gated = keep.tile([P, HALF], F32, name=f"gated{h}{b}")
+            nc.scalar.copy(out=gated[:], in_=turned[:].rearrange("p c t -> p (c t)"))
+            return gated
+
+        early = [psum.tile([P, 1, P], F32, name=f"early{c}", tag=f"early{c}") for c in range(2)]
+        third = [psum.tile([P, 1, P], F32, name=f"third{c}", tag=f"third{c}") for c in range(2)]
+        for c in range(2):
+            product(early[c][:, 0, :], 0, c, 1)
+        for c in range(2):
+            product(third[c][:, 0, :], 0, 2 + c, 0)
+        first = psum.tile([P, 2, P], F32, name="first")
+        for c in range(2):
+            toks = slice(P * c, P * (c + 1))
+            for z in range(PASSES):
+                nc.tensor.matmul_mx(
+                    out=first[:, c, :],
+                    lhsT=w_words[z][:, 0 : 2 * P].bitcast(FP4X4), lhsT_scale=w_scales[:, z * N : z * N + P],
+                    rhs=[codes0, codes1][z][0][:, toks].bitcast(FP8X4), rhs_scale=[scales0, scales1][z][0][:, toks],
+                    start=(z == 0), stop=(z == PASSES - 1),
                 )
-                nc.tensor.transpose(turned[:, c, :], scaled[:], identity[:])
-            nc.scalar.copy(out=gated[1][:, HALF * h : HALF * (h + 1)], in_=turned[:].rearrange("p c t -> p (c t)"))
-        for b in range(BLOCKS):
-            nc.vector.tensor_tensor(windows[b][:].indirect(offsets[:]), olds[b][:], gated[b][:], ALU.add)
-            nc.sync.dma_start(out=out[P * b : P * (b + 1), :], in_=windows[b][:])
+        for c in range(2):
+            product(early[c][:, 0, :], 1, c, 1)
+
+        gated_first = keep.tile([P, HALF], F32, name="gated_first")
+        nc.vector.scalar_tensor_tensor(
+            out=gated_first[:], in0=first[:].rearrange("p c t -> p (c t)"), scalar=0.0, in1=gate_rows[:],
+            op0=ALU.max, op1=ALU.mult,
+        )
+        pick_old1(1, "codes1_0")
+        scatter(gated_first, 0, 0)
+        scatter(gate_on_scalar([early[0][:], early[1][:]], 0, 1, "turned01"), 0, 1)
+        for c in range(2):
+            product(third[c][:, 0, :], 1, 2 + c, 0)
+        scatter(gate_on_scalar([third[0][:], third[1][:]], 1, 0, "turned10"), 1, 0)
+        nc.sync.dma_start(out=out[0:P, :], in_=windows[0][:])
+        last = psum.tile([P, 2, P], F32, name="last", tag="third1")
+        for c in range(2):
+            for z in range(PASSES):
+                product(last[:, c, :], z, 2 + c, 1)
+        scatter(gate_on_scalar([last[:]], 1, 1, "turned11"), 1, 1)
+        nc.sync.dma_start(out=out[P : 2 * P, :], in_=windows[1][:])

@@ -43,13 +43,12 @@ def tile_picked_modres_linrelu_l_kernel(tc, xT, gate, res, w1_words, w1_scales, 
         nc.gpsimd.memset(w_scales[:].bitcast(I32), 0)
         gate_chunks = keep.tile([P, P], F32, name="gate_chunks")
         nc.gpsimd.memset(gate_chunks[:], 0.0)
-        nc.gpsimd.dma_start(out=gate_chunks[0 : S // P, :], in_=gate[0, :].rearrange("(c p) -> c p", p=P))
         for q in range(4):
-            queue = nc.scalar if q < 2 else nc.gpsimd
-            queue.dma_start(
+            nc.gpsimd.dma_start(
                 out=w_scales[32 * q : 32 * q + 4, :].rearrange("r (z c) -> r z c", z=PASSES).bitcast(I32),
                 in_=w1_scales[:, 4 * q : 4 * q + 4, :].rearrange("z r c -> r z c").bitcast(I32),
             )
+        nc.gpsimd.dma_start(out=gate_chunks[0 : S // P, :], in_=gate[0, :].rearrange("(c p) -> c p", p=P))
         identity = keep.tile([P, P], F32, name="identity")
         make_identity(nc, identity[:])
 
@@ -117,21 +116,22 @@ def tile_picked_modres_linrelu_l_kernel(tc, xT, gate, res, w1_words, w1_scales, 
 
         codes1 = [keep.tile([P, HALF], U32, name=f"codes1_{h}", tag=f"codes1_{h}", align_bytes=64) for h in range(2)]
         scales1 = [keep.tile([P, HALF], U8, name=f"scales1_{h}", align_bytes=64) for h in range(2)]
-        old0 = keep.tile([P, S], F32, name="old0")
-        olds = {(0, 0): old0[:, 0:HALF], (1, 0): old0[:, HALF:S]}
 
-        def pick_old1(h, tag):
-            old = keep.tile([P, HALF], F32, name=f"old1_{h}", tag=tag, align_bytes=64)
-            nc.vector.tensor_copy(old[:], windows[1][:].indirect(half_list(h)))
-            olds[(h, 1)] = old[:]
+        def chunks_list(c0, count):
+            return offsets[:, 8 * c0 : 8 * (c0 + count)]
 
-        pick_old1(0, "old1_0")
+        def pick_old(b, c0, count, tag):
+            old = keep.tile([P, count * P], F32, name=f"old{b}_{c0}", tag=tag, align_bytes=64)
+            nc.vector.tensor_copy(old[:], windows[b][:].indirect(chunks_list(c0, count)))
+            return old
+
+        old1_rest = pick_old(1, 1, 3, "old1_rest")
         for h in range(2):
             nc.vector.quantize_mx(
                 out=codes1[h][:].bitcast(FP8X4), scales=scales1[h][:],
                 in_=quads1[h][:].rearrange("p s u -> p (s u)").bitcast(BF16),
             )
-        nc.vector.tensor_copy(old0[:], windows[0][:].indirect(offsets[:]))
+        old0 = pick_old(0, 0, 4, "old0")
 
         def product(acc, z, c, b):
             toks = slice(P * (c % 2), P * (c % 2 + 1))
@@ -143,32 +143,30 @@ def tile_picked_modres_linrelu_l_kernel(tc, xT, gate, res, w1_words, w1_scales, 
                 start=(z == 0), stop=(z == PASSES - 1),
             )
 
-        def scatter(gated, h, b):
-            nc.vector.tensor_tensor(
-                windows[b][:].indirect(half_list(h)), olds[(h, b)], gated[:], ALU.add
-            )
+        def scatter(b, c0, count, old, gated):
+            nc.vector.tensor_tensor(windows[b][:].indirect(chunks_list(c0, count)), old, gated[:], ALU.add)
 
-        def gate_on_scalar(sums, h, b, bank):
-            turned = psum.tile([P, 2, P], F32, name=f"turned{h}{b}", tag=bank)
+        def gate_on_scalar(sums, c0, b, bank):
+            count = sum(acc.shape[1] for acc in sums)
+            turned = psum.tile([P, count, P], F32, name=f"turned{c0}{b}", tag=bank)
             c = 0
             for acc in sums:
-                active = keep.tile([P, acc.shape[1], P], F32, name=f"active{h}{b}{c}")
+                active = keep.tile([P, acc.shape[1], P], F32, name=f"active{c0 + c}{b}")
                 nc.scalar.activation(out=active[:], in_=acc, func=ACT.Relu)
                 for j in range(acc.shape[1]):
-                    scaled = keep.tile([P, P], F32, name=f"scaled{h}{b}{c}")
+                    scaled = keep.tile([P, P], F32, name=f"scaled{c0 + c}{b}")
                     nc.scalar.activation(
-                        out=scaled[:], in_=active[:, j, :], func=ACT.Copy, scale=gates[:, 2 * h + c : 2 * h + c + 1]
+                        out=scaled[:], in_=active[:, j, :], func=ACT.Copy, scale=gates[:, c0 + c : c0 + c + 1]
                     )
                     nc.tensor.transpose(turned[:, c, :], scaled[:], identity[:])
                     c = c + 1
-            gated = keep.tile([P, HALF], F32, name=f"gated{h}{b}")
+            gated = keep.tile([P, count * P], F32, name=f"gated{c0}{b}")
             nc.scalar.copy(out=gated[:], in_=turned[:].rearrange("p c t -> p (c t)"))
             return gated
 
-        early = [psum.tile([P, 1, P], F32, name=f"early{c}", tag=f"early{c}") for c in range(2)]
+        second = psum.tile([P, 1, P], F32, name="second")
         third = [psum.tile([P, 1, P], F32, name=f"third{c}", tag=f"third{c}") for c in range(2)]
-        for c in range(2):
-            product(early[c][:, 0, :], 0, c, 1)
+        product(second[:, 0, :], 0, 0, 1)
         for c in range(2):
             product(third[c][:, 0, :], 0, 2 + c, 0)
         first = psum.tile([P, 2, P], F32, name="first")
@@ -181,24 +179,25 @@ def tile_picked_modres_linrelu_l_kernel(tc, xT, gate, res, w1_words, w1_scales, 
                     rhs=[codes0, codes1][z][0][:, toks].bitcast(FP8X4), rhs_scale=[scales0, scales1][z][0][:, toks],
                     start=(z == 0), stop=(z == PASSES - 1),
                 )
-        for c in range(2):
-            product(early[c][:, 0, :], 1, c, 1)
+        product(second[:, 0, :], 1, 0, 1)
+        last = psum.tile([P, 3, P], F32, name="last")
+        for z in range(PASSES):
+            product(last[:, 0, :], z, 1, 1)
 
         gated_first = keep.tile([P, HALF], F32, name="gated_first")
         nc.vector.scalar_tensor_tensor(
             out=gated_first[:], in0=first[:].rearrange("p c t -> p (c t)"), scalar=0.0, in1=gate_rows[:],
             op0=ALU.max, op1=ALU.mult,
         )
-        pick_old1(1, "codes1_0")
-        scatter(gated_first, 0, 0)
-        scatter(gate_on_scalar([early[0][:], early[1][:]], 0, 1, "turned01"), 0, 1)
+        old1_first = pick_old(1, 0, 1, "codes1_0")
+        scatter(0, 0, 2, old0[:, 0:HALF], gated_first)
+        scatter(1, 0, 1, old1_first[:], gate_on_scalar([second[:]], 0, 1, "turned01"))
         for c in range(2):
             product(third[c][:, 0, :], 1, 2 + c, 0)
-        scatter(gate_on_scalar([third[0][:], third[1][:]], 1, 0, "turned10"), 1, 0)
+        scatter(0, 2, 2, old0[:, HALF:S], gate_on_scalar([third[0][:], third[1][:]], 2, 0, "turned20"))
         nc.sync.dma_start(out=out[0:P, :], in_=windows[0][:])
-        last = psum.tile([P, 2, P], F32, name="last", tag="third1")
         for c in range(2):
             for z in range(PASSES):
-                product(last[:, c, :], z, 2 + c, 1)
-        scatter(gate_on_scalar([last[:]], 1, 1, "turned11"), 1, 1)
+                product(last[:, 1 + c, :], z, 2 + c, 1)
+        scatter(1, 1, 3, old1_rest[:], gate_on_scalar([last[:]], 1, 1, "turned11"))
         nc.sync.dma_start(out=out[P : 2 * P, :], in_=windows[1][:])

@@ -23,7 +23,7 @@ BLOCKS = 2
 HALF = S // 2
 
 CHUNKS = [
-    [(0, 512, 512), (512, 1024, 256)],
+    [(0, 1024, 416)],
     [(0, 512, 512), (512, 1024, 320)],
     [(0, 512, 512), (512, 1024, 256)],
     [(0, 512, 512), (512, 1024, 192)],
@@ -43,14 +43,15 @@ def tile_picked_modres_linrelu_l_kernel(tc, xT, gate, res, w1_words, w1_scales, 
         nc.gpsimd.memset(w_scales[:].bitcast(I32), 0)
         gate_chunks = keep.tile([P, P], F32, name="gate_chunks")
         nc.gpsimd.memset(gate_chunks[:], 0.0)
+        identity = keep.tile([P, P], F32, name="identity")
+        make_identity(nc, identity[:])
         for q in range(4):
-            nc.gpsimd.dma_start(
+            queue = nc.scalar if q == 0 else nc.gpsimd
+            queue.dma_start(
                 out=w_scales[32 * q : 32 * q + 4, :].rearrange("r (z c) -> r z c", z=PASSES).bitcast(I32),
                 in_=w1_scales[:, 4 * q : 4 * q + 4, :].rearrange("z r c -> r z c").bitcast(I32),
             )
         nc.gpsimd.dma_start(out=gate_chunks[0 : S // P, :], in_=gate[0, :].rearrange("(c p) -> c p", p=P))
-        identity = keep.tile([P, P], F32, name="identity")
-        make_identity(nc, identity[:])
 
         raws = []
         for i in range(4):

@@ -21,6 +21,7 @@ P = 128
 PASSES = 2
 BLOCKS = 2
 HALF = S // 2
+LEAD = 192
 
 CHUNKS = [
     [(0, 1024, 416)],
@@ -51,7 +52,7 @@ def tile_picked_modres_linrelu_l_kernel(tc, xT, gate, res, w1_words, w1_scales, 
                 out=w_scales[32 * q : 32 * q + 4, :].rearrange("r (z c) -> r z c", z=PASSES).bitcast(I32),
                 in_=w1_scales[:, 4 * q : 4 * q + 4, :].rearrange("z r c -> r z c").bitcast(I32),
             )
-        nc.gpsimd.dma_start(out=gate_chunks[0 : S // P, :], in_=gate[0, :].rearrange("(c p) -> c p", p=P))
+        nc.scalar.dma_start(out=gate_chunks[0 : S // P, :], in_=gate[0, :].rearrange("(c p) -> c p", p=P))
 
         raws = []
         for i in range(4):
@@ -64,14 +65,17 @@ def tile_picked_modres_linrelu_l_kernel(tc, xT, gate, res, w1_words, w1_scales, 
                     nc.sync.dma_start(offsets[:], offs)
             raws.append(row)
 
-        w_words = [keep.tile([P, 2 * N], U8, name=f"w_words{z}", align_bytes=64) for z in range(PASSES)]
+        w_both = keep.tile([P, PASSES * 2 * N], U8, name="w_both", align_bytes=64)
+        w_words = [w_both[:, 2 * N * z : 2 * N * (z + 1)] for z in range(PASSES)]
         windows = [keep.tile([P, T], F32, name=f"res{b}") for b in range(BLOCKS)]
         nc.sync.dma_start(out=windows[1][:], in_=res[P : 2 * P, :])
-        nc.sync.dma_start(out=w_words[0][:].bitcast(I32), in_=w1_words[0].bitcast(I32))
+        nc.sync.dma_start(
+            out=w_both[:].rearrange("p (z c) -> p z c", z=PASSES).bitcast(I32),
+            in_=w1_words.rearrange("z p c -> p z c").bitcast(I32),
+        )
         nc.sync.dma_start(out=windows[0][:], in_=res[0:P, :])
         gate_rows = keep.tile([P, HALF], F32, name="gate_rows")
         nc.sync.dma_start(out=gate_rows[:], in_=gate[:, 0:HALF])
-        nc.sync.dma_start(out=w_words[1][:].bitcast(I32), in_=w1_words[1].bitcast(I32))
 
         gates_turned = psum.tile([P, P], F32, name="gates_turned", tag="turned01")
         nc.tensor.transpose(gates_turned[:], gate_chunks[:], identity[:])
@@ -118,21 +122,23 @@ def tile_picked_modres_linrelu_l_kernel(tc, xT, gate, res, w1_words, w1_scales, 
         codes1 = [keep.tile([P, HALF], U32, name=f"codes1_{h}", tag=f"codes1_{h}", align_bytes=64) for h in range(2)]
         scales1 = [keep.tile([P, HALF], U8, name=f"scales1_{h}", align_bytes=64) for h in range(2)]
 
-        def chunks_list(c0, count):
-            return offsets[:, 8 * c0 : 8 * (c0 + count)]
+        def entries(j0, j1):
+            return offsets[:, j0 // 16 : j1 // 16]
 
-        def pick_old(b, c0, count, tag):
-            old = keep.tile([P, count * P], F32, name=f"old{b}_{c0}", tag=tag, align_bytes=64)
-            nc.vector.tensor_copy(old[:], windows[b][:].indirect(chunks_list(c0, count)))
-            return old
-
-        old1_rest = pick_old(1, 1, 3, "old1_rest")
+        old1 = [
+            keep.tile([P, LEAD], F32, name="old1_lead", align_bytes=64),
+            keep.tile([P, S - LEAD], F32, name="old1_rest", tag="picked1_0", align_bytes=64),
+        ]
+        nc.vector.tensor_copy(old1[0][:], windows[1][:].indirect(entries(0, LEAD)))
         for h in range(2):
             nc.vector.quantize_mx(
                 out=codes1[h][:].bitcast(FP8X4), scales=scales1[h][:],
                 in_=quads1[h][:].rearrange("p s u -> p (s u)").bitcast(BF16),
             )
-        old0 = pick_old(0, 0, 4, "old0")
+            if h == 0:
+                nc.vector.tensor_copy(old1[1][:], windows[1][:].indirect(entries(LEAD, S)))
+        old0 = keep.tile([P, S], F32, name="old0", align_bytes=64)
+        nc.vector.tensor_copy(old0[:], windows[0][:].indirect(entries(0, S)))
 
         def product(acc, z, c, b):
             toks = slice(P * (c % 2), P * (c % 2 + 1))
@@ -144,61 +150,52 @@ def tile_picked_modres_linrelu_l_kernel(tc, xT, gate, res, w1_words, w1_scales, 
                 start=(z == 0), stop=(z == PASSES - 1),
             )
 
-        def scatter(b, c0, count, old, gated):
-            nc.vector.tensor_tensor(windows[b][:].indirect(chunks_list(c0, count)), old, gated[:], ALU.add)
+        def scatter(b, j0, j1, old, gated):
+            nc.vector.tensor_tensor(windows[b][:].indirect(entries(j0, j1)), old, gated, ALU.add)
 
-        def gate_on_scalar(sums, c0, b, bank):
-            count = sum(acc.shape[1] for acc in sums)
+        def gate_on_scalar(acc, c0, b, bank, gated):
+            count = acc.shape[1]
             turned = psum.tile([P, count, P], F32, name=f"turned{c0}{b}", tag=bank)
-            c = 0
-            for acc in sums:
-                active = keep.tile([P, acc.shape[1], P], F32, name=f"active{c0 + c}{b}")
-                nc.scalar.activation(out=active[:], in_=acc, func=ACT.Relu)
-                for j in range(acc.shape[1]):
-                    scaled = keep.tile([P, P], F32, name=f"scaled{c0 + c}{b}")
-                    nc.scalar.activation(
-                        out=scaled[:], in_=active[:, j, :], func=ACT.Copy, scale=gates[:, c0 + c : c0 + c + 1]
-                    )
-                    nc.tensor.transpose(turned[:, c, :], scaled[:], identity[:])
-                    c = c + 1
-            gated = keep.tile([P, count * P], F32, name=f"gated{c0}{b}")
-            nc.scalar.copy(out=gated[:], in_=turned[:].rearrange("p c t -> p (c t)"))
-            return gated
+            active = keep.tile([P, count, P], F32, name=f"active{c0}{b}")
+            nc.scalar.activation(out=active[:], in_=acc, func=ACT.Relu)
+            for j in range(count):
+                scaled = keep.tile([P, P], F32, name=f"scaled{c0 + j}{b}")
+                nc.scalar.activation(
+                    out=scaled[:], in_=active[:, j, :], func=ACT.Copy, scale=gates[:, c0 + j : c0 + j + 1]
+                )
+                nc.tensor.transpose(turned[:, j, :], scaled[:], identity[:])
+            nc.scalar.copy(out=gated, in_=turned[:].rearrange("p c t -> p (c t)"))
 
-        second = psum.tile([P, 1, P], F32, name="second")
-        third = [psum.tile([P, 1, P], F32, name=f"third{c}", tag=f"third{c}") for c in range(2)]
-        product(second[:, 0, :], 0, 0, 1)
-        for c in range(2):
-            product(third[c][:, 0, :], 0, 2 + c, 0)
-        first = psum.tile([P, 2, P], F32, name="first")
-        for c in range(2):
-            toks = slice(P * c, P * (c + 1))
-            for z in range(PASSES):
+        gated = [keep.tile([P, S], F32, name=f"gated{b}") for b in range(BLOCKS)]
+        first = [psum.tile([P, P], F32, name=f"first{c}") for c in range(2)]
+        for z in range(PASSES):
+            for c in range(2):
+                toks = slice(P * c, P * (c + 1))
                 nc.tensor.matmul_mx(
-                    out=first[:, c, :],
+                    out=first[c][:],
                     lhsT=w_words[z][:, 0 : 2 * P].bitcast(FP4X4), lhsT_scale=w_scales[:, z * N : z * N + P],
                     rhs=[codes0, codes1][z][0][:, toks].bitcast(FP8X4), rhs_scale=[scales0, scales1][z][0][:, toks],
                     start=(z == 0), stop=(z == PASSES - 1),
                 )
-        product(second[:, 0, :], 1, 0, 1)
-        last = psum.tile([P, 3, P], F32, name="last")
-        for z in range(PASSES):
-            product(last[:, 0, :], z, 1, 1)
+        for c in range(2):
+            toks = slice(P * c, P * (c + 1))
+            active_first = keep.tile([P, P], F32, name=f"active_first{c}")
+            nc.scalar.activation(out=active_first[:], in_=first[c][:], func=ACT.Relu)
+            nc.gpsimd.tensor_tensor(gated[0][:, toks], active_first[:], gate_rows[:, toks], ALU.mult)
+        scatter(0, 0, HALF, old0[:, 0:HALF], gated[0][:, 0:HALF])
 
-        gated_first = keep.tile([P, HALF], F32, name="gated_first")
-        nc.vector.scalar_tensor_tensor(
-            out=gated_first[:], in0=first[:].rearrange("p c t -> p (c t)"), scalar=0.0, in1=gate_rows[:],
-            op0=ALU.max, op1=ALU.mult,
-        )
-        old1_first = pick_old(1, 0, 1, "codes1_0")
-        scatter(0, 0, 2, old0[:, 0:HALF], gated_first)
-        scatter(1, 0, 1, old1_first[:], gate_on_scalar([second[:]], 0, 1, "turned01"))
-        for c in range(2):
-            product(third[c][:, 0, :], 1, 2 + c, 0)
-        scatter(0, 2, 2, old0[:, HALF:S], gate_on_scalar([third[0][:], third[1][:]], 2, 0, "turned20"))
+        def piece(c0, b, bank):
+            acc = psum.tile([P, 2, P], F32, name=f"acc{c0}{b}")
+            for c in range(2):
+                for z in range(PASSES):
+                    product(acc[:, c, :], z, c0 + c, b)
+            gate_on_scalar(acc[:], c0, b, bank, gated[b][:, P * c0 : P * (c0 + 2)])
+
+        piece(0, 1, "turned01")
+        scatter(1, 0, LEAD, old1[0][:], gated[1][:, 0:LEAD])
+        piece(2, 0, "turned20")
+        scatter(0, HALF, S, old0[:, HALF:S], gated[0][:, HALF:S])
         nc.sync.dma_start(out=out[0:P, :], in_=windows[0][:])
-        for c in range(2):
-            for z in range(PASSES):
-                product(last[:, 1 + c, :], z, 2 + c, 1)
-        scatter(1, 1, 3, old1_rest[:], gate_on_scalar([last[:]], 1, 1, "turned11"))
+        piece(2, 1, "turned21")
+        scatter(1, LEAD, S, old1[1][:], gated[1][:, LEAD:S])
         nc.sync.dma_start(out=out[P : 2 * P, :], in_=windows[1][:])

@@ -21,7 +21,7 @@ P = 128
 PASSES = 2
 BLOCKS = 2
 HALF = S // 2
-LEAD = 192
+LAST_PIECES = [(0, P), (P, HALF), (HALF, S)]
 
 CHUNKS = [
     [(0, 1024, 416)],
@@ -100,9 +100,7 @@ def tile_picked_modres_linrelu_l_kernel(tc, xT, gate, res, w1_words, w1_scales, 
             nc.vector.tensor_copy(quads0[:, :, u], pairs[:].indirect(offsets[:]))
 
         codes0, scales0 = [], []
-        picked1 = [
-            keep.tile([P, 2, HALF], U32, name=f"picked1_{h}", tag=f"picked1_{h}", align_bytes=64) for h in range(2)
-        ]
+        picked1 = keep.tile([P, 2, S], U32, name="picked1", align_bytes=64)
         for u in range(2):
             pairs = cast(2 + u)
             codes0.append(keep.tile([P, HALF], U32, name=f"codes0_{u}", tag=f"raw{2 + u}_0", align_bytes=64))
@@ -111,12 +109,15 @@ def tile_picked_modres_linrelu_l_kernel(tc, xT, gate, res, w1_words, w1_scales, 
                 out=codes0[u][:].bitcast(FP8X4), scales=scales0[u][:],
                 in_=quads0[:, HALF * u : HALF * (u + 1), :].rearrange("p s u -> p (s u)").bitcast(BF16),
             )
-            for h in range(2):
-                nc.vector.tensor_copy(picked1[h][:, u, :], pairs[:].indirect(half_list(h)))
-        quads1 = [keep.tile([P, HALF, 2], U32, name=f"quads1_{h}", align_bytes=64) for h in range(2)]
-        for h in range(2):
-            nc.scalar.copy(out=quads1[h][:], in_=picked1[h][:].rearrange("p u s -> p s u"))
-        gates = keep.tile([P, S // P], F32, name="gates", tag="picked1_1", align_bytes=64)
+            for j0, j1 in ([(0, S)], LAST_PIECES)[u]:
+                nc.vector.tensor_copy(picked1[:, u, j0:j1], pairs[:].indirect(offsets[:, j0 // 16 : j1 // 16]))
+        quads1 = [keep.tile([P, HALF, 2], U32, name=f"quads1_{h}", tag=f"quads1_{h}", align_bytes=64) for h in range(2)]
+        for j0, j1 in LAST_PIECES:
+            h = j0 // HALF
+            nc.scalar.copy(
+                out=quads1[h][:, j0 - HALF * h : j1 - HALF * h, :], in_=picked1[:, :, j0:j1].rearrange("p u s -> p s u")
+            )
+        gates = keep.tile([P, S // P], F32, name="gates", tag="raw1_1", align_bytes=64)
         nc.scalar.copy(out=gates[:], in_=gates_turned[:, 0 : S // P])
 
         codes1 = [keep.tile([P, HALF], U32, name=f"codes1_{h}", tag=f"codes1_{h}", align_bytes=64) for h in range(2)]
@@ -125,18 +126,13 @@ def tile_picked_modres_linrelu_l_kernel(tc, xT, gate, res, w1_words, w1_scales, 
         def entries(j0, j1):
             return offsets[:, j0 // 16 : j1 // 16]
 
-        old1 = [
-            keep.tile([P, LEAD], F32, name="old1_lead", align_bytes=64),
-            keep.tile([P, S - LEAD], F32, name="old1_rest", tag="picked1_0", align_bytes=64),
-        ]
-        nc.vector.tensor_copy(old1[0][:], windows[1][:].indirect(entries(0, LEAD)))
+        old1 = [picked1[:, 0, HALF * h : HALF * (h + 1)].bitcast(F32) for h in range(2)]
         for h in range(2):
             nc.vector.quantize_mx(
                 out=codes1[h][:].bitcast(FP8X4), scales=scales1[h][:],
                 in_=quads1[h][:].rearrange("p s u -> p (s u)").bitcast(BF16),
             )
-            if h == 0:
-                nc.vector.tensor_copy(old1[1][:], windows[1][:].indirect(entries(LEAD, S)))
+            nc.vector.tensor_copy(old1[h], windows[1][:].indirect(half_list(h)))
         old0 = keep.tile([P, S], F32, name="old0", align_bytes=64)
         nc.vector.tensor_copy(old0[:], windows[0][:].indirect(entries(0, S)))
 
@@ -153,49 +149,53 @@ def tile_picked_modres_linrelu_l_kernel(tc, xT, gate, res, w1_words, w1_scales, 
         def scatter(b, j0, j1, old, gated):
             nc.vector.tensor_tensor(windows[b][:].indirect(entries(j0, j1)), old, gated, ALU.add)
 
-        def gate_on_scalar(acc, c0, b, bank, gated):
-            count = acc.shape[1]
-            turned = psum.tile([P, count, P], F32, name=f"turned{c0}{b}", tag=bank)
-            active = keep.tile([P, count, P], F32, name=f"active{c0}{b}")
-            nc.scalar.activation(out=active[:], in_=acc, func=ACT.Relu)
-            for j in range(count):
+        def gate_on_scalar(sums, c0, b, bank, active_tag):
+            turned = psum.tile([P, 2, P], F32, name=f"turned{c0}{b}", tag=bank)
+            active = keep.tile([P, 2, P], F32, name=f"active{c0}{b}", tag=active_tag)
+            c = 0
+            for acc in sums:
+                nc.scalar.activation(out=active[:, c : c + acc.shape[1], :], in_=acc, func=ACT.Relu)
+                c = c + acc.shape[1]
+            for j in range(2):
                 scaled = keep.tile([P, P], F32, name=f"scaled{c0 + j}{b}")
                 nc.scalar.activation(
                     out=scaled[:], in_=active[:, j, :], func=ACT.Copy, scale=gates[:, c0 + j : c0 + j + 1]
                 )
                 nc.tensor.transpose(turned[:, j, :], scaled[:], identity[:])
-            nc.scalar.copy(out=gated, in_=turned[:].rearrange("p c t -> p (c t)"))
+            gated = keep.tile([P, HALF], F32, name=f"gated{c0}{b}")
+            nc.scalar.copy(out=gated[:], in_=turned[:].rearrange("p c t -> p (c t)"))
+            return gated
 
-        gated = [keep.tile([P, S], F32, name=f"gated{b}") for b in range(BLOCKS)]
-        first = [psum.tile([P, P], F32, name=f"first{c}") for c in range(2)]
+        first = [psum.tile([P, P], F32, name=f"first{c}", tag=f"first{c}") for c in range(2)]
+        second = [psum.tile([P, 1, P], F32, name=f"second{c}") for c in range(2)]
         for z in range(PASSES):
             for c in range(2):
                 toks = slice(P * c, P * (c + 1))
                 nc.tensor.matmul_mx(
                     out=first[c][:],
-                    lhsT=w_words[z][:, 0 : 2 * P].bitcast(FP4X4), lhsT_scale=w_scales[:, z * N : z * N + P],
+                    lhsT=w_words[z][:, 2 * P : 4 * P].bitcast(FP4X4), lhsT_scale=w_scales[:, z * N + P : z * N + 2 * P],
                     rhs=[codes0, codes1][z][0][:, toks].bitcast(FP8X4), rhs_scale=[scales0, scales1][z][0][:, toks],
                     start=(z == 0), stop=(z == PASSES - 1),
                 )
+            for c in range(2):
+                product(second[c][:, 0, :], z, c, 0)
+        gated_first = keep.tile([P, HALF], F32, name="gated_first", tag="quads1_1", align_bytes=64)
         for c in range(2):
             toks = slice(P * c, P * (c + 1))
             active_first = keep.tile([P, P], F32, name=f"active_first{c}")
             nc.scalar.activation(out=active_first[:], in_=first[c][:], func=ACT.Relu)
-            nc.gpsimd.tensor_tensor(gated[0][:, toks], active_first[:], gate_rows[:, toks], ALU.mult)
-        scatter(0, 0, HALF, old0[:, 0:HALF], gated[0][:, 0:HALF])
+            nc.gpsimd.tensor_tensor(gated_first[:, toks], active_first[:], gate_rows[:, toks], ALU.mult)
+        scatter(1, 0, HALF, old1[0], gated_first[:])
+        scatter(0, 0, HALF, old0[:, 0:HALF], gate_on_scalar([second[0][:], second[1][:]], 0, 0, "turned01", "active")[:])
 
-        def piece(c0, b, bank):
-            acc = psum.tile([P, 2, P], F32, name=f"acc{c0}{b}")
+        def piece(c0, b, acc_bank, bank, active_tag):
+            acc = psum.tile([P, 2, P], F32, name=f"acc{c0}{b}", tag=acc_bank)
             for c in range(2):
                 for z in range(PASSES):
                     product(acc[:, c, :], z, c0 + c, b)
-            gate_on_scalar(acc[:], c0, b, bank, gated[b][:, P * c0 : P * (c0 + 2)])
+            return gate_on_scalar([acc[:]], c0, b, bank, active_tag)
 
-        piece(0, 1, "turned01")
-        scatter(1, 0, LEAD, old1[0][:], gated[1][:, 0:LEAD])
-        piece(2, 0, "turned20")
-        scatter(0, HALF, S, old0[:, HALF:S], gated[0][:, HALF:S])
-        nc.sync.dma_start(out=out[0:P, :], in_=windows[0][:])
-        piece(2, 1, "turned21")
-        scatter(1, LEAD, S, old1[1][:], gated[1][:, LEAD:S])
+        scatter(1, HALF, S, old1[1], piece(2, 1, "first0", "turned21", "active")[:])
         nc.sync.dma_start(out=out[P : 2 * P, :], in_=windows[1][:])
+        scatter(0, HALF, S, old0[:, HALF:S], piece(2, 0, "first1", "turned20", "active")[:])
+        nc.sync.dma_start(out=out[0:P, :], in_=windows[0][:])

@@ -18,17 +18,10 @@ ALU = mybir.AluOpType
 ACT = mybir.ActivationFunctionType
 
 P = 128
+PACK = 4
 PASSES = 2
 BLOCKS = 2
 HALF = S // 2
-LAST_PIECES = [(0, P), (P, HALF), (HALF, S)]
-
-CHUNKS = [
-    [(0, 1024, 416)],
-    [(0, 512, 512), (512, 1024, 320)],
-    [(0, 512, 512), (512, 1024, 256)],
-    [(0, 512, 512), (512, 1024, 192)],
-]
 
 
 def tile_picked_modres_linrelu_l_kernel(tc, xT, gate, res, w1_words, w1_scales, offs, out):
@@ -38,164 +31,127 @@ def tile_picked_modres_linrelu_l_kernel(tc, xT, gate, res, w1_words, w1_scales, 
         psum = ctx.enter_context(tc.psum_pool(name="psum", bufs=1))
 
         offsets = keep.tile([P, S // 16], U16, name="offsets")
-        x_rows = xT.rearrange("(z p u e) t -> z u p e t", z=PASSES, p=P, u=2, e=2)
+        x_rows = xT.rearrange("(z p t) c -> z t p c", z=PASSES, p=P, t=PACK)
 
         w_scales = keep.tile([P, PASSES * N], U8, name="w_scales", align_bytes=64)
         nc.gpsimd.memset(w_scales[:].bitcast(I32), 0)
+        warm = keep.tile([P, 8], F32, name="warm")
+        nc.vector.memset(warm[:, 0:1], 0.0)
+        nc.scalar.activation(out=warm[:, 4:5], in_=warm[:, 0:1], func=ACT.Copy)
         gate_chunks = keep.tile([P, P], F32, name="gate_chunks")
         nc.gpsimd.memset(gate_chunks[:], 0.0)
+        nc.scalar.dma_start(out=gate_chunks[0 : S // P, :], in_=gate[0, :].rearrange("(c p) -> c p", p=P))
         identity = keep.tile([P, P], F32, name="identity")
         make_identity(nc, identity[:])
         for q in range(4):
-            queue = nc.scalar if q == 0 else nc.gpsimd
+            queue = nc.scalar if q < 2 else nc.gpsimd
             queue.dma_start(
                 out=w_scales[32 * q : 32 * q + 4, :].rearrange("r (z c) -> r z c", z=PASSES).bitcast(I32),
                 in_=w1_scales[:, 4 * q : 4 * q + 4, :].rearrange("z r c -> r z c").bitcast(I32),
             )
-        nc.scalar.dma_start(out=gate_chunks[0 : S // P, :], in_=gate[0, :].rearrange("(c p) -> c p", p=P))
 
-        raws = []
-        for i in range(4):
-            row = []
-            for c, (c0, c1, unused) in enumerate(CHUNKS[i]):
-                raw = keep.tile([P, 2, c1 - c0], F32, name=f"raw{i}_{c}", tag=f"raw{i}_{c}", align_bytes=64)
-                nc.sync.dma_start(out=raw[:], in_=x_rows[i // 2, i % 2][:, :, c0:c1])
-                row.append(raw)
-                if i == 0 and c == 0:
-                    nc.sync.dma_start(offsets[:], offs)
-            raws.append(row)
+        w_words = [keep.tile([P, 2 * N], U8, name=f"w_words{z}", align_bytes=64) for z in range(PASSES)]
+        planes = []
+        for i in range(PASSES * PACK):
+            plane = keep.tile([P, T], F32, name=f"plane{i}")
+            nc.sync.dma_start(out=plane[:], in_=x_rows[i // PACK, i % PACK])
+            planes.append(plane)
+            if i == 0:
+                nc.sync.dma_start(offsets[:], offs)
+            if i == 5:
+                nc.sync.dma_start(out=w_words[0][:].bitcast(I32), in_=w1_words[0].bitcast(I32))
 
-        w_both = keep.tile([P, PASSES * 2 * N], U8, name="w_both", align_bytes=64)
-        w_words = [w_both[:, 2 * N * z : 2 * N * (z + 1)] for z in range(PASSES)]
         windows = [keep.tile([P, T], F32, name=f"res{b}") for b in range(BLOCKS)]
         nc.sync.dma_start(out=windows[1][:], in_=res[P : 2 * P, :])
-        nc.sync.dma_start(
-            out=w_both[:].rearrange("p (z c) -> p z c", z=PASSES).bitcast(I32),
-            in_=w1_words.rearrange("z p c -> p z c").bitcast(I32),
-        )
+        nc.sync.dma_start(out=w_words[1][:].bitcast(I32), in_=w1_words[1].bitcast(I32))
         nc.sync.dma_start(out=windows[0][:], in_=res[0:P, :])
-        gate_rows = keep.tile([P, HALF], F32, name="gate_rows")
-        nc.sync.dma_start(out=gate_rows[:], in_=gate[:, 0:HALF])
 
-        gates_turned = psum.tile([P, P], F32, name="gates_turned", tag="turned01")
+        gates_turned = psum.tile([P, P], F32, name="gates_turned")
         nc.tensor.transpose(gates_turned[:], gate_chunks[:], identity[:])
-
-        def cast(i):
-            pairs = keep.tile([P, T], U32, name=f"pairs{i}", tag=f"pairs{i}")
-            view = pairs[:].bitcast(BF16).rearrange("p (t e) -> p t e", e=2)
-            for raw, (c0, c1, share) in zip(raws[i], CHUNKS[i]):
-                src = raw[:].rearrange("p e t -> p t e")
-                if share > 0:
-                    nc.scalar.copy(out=view[:, c0 : c0 + share, :], in_=src[:, 0:share, :])
-                if c0 + share < c1:
-                    nc.vector.tensor_copy(out=view[:, c0 + share : c1, :], in_=src[:, share:, :])
-            return pairs
+        gate_columns = keep.tile([P, S // P], F32, name="gate_columns")
+        nc.scalar.copy(out=gate_columns[:], in_=gates_turned[:, 0 : S // P])
+        gates_spread = psum.tile([P, S], F32, name="gates_spread")
+        for c in range(S // P):
+            nc.tensor.transpose(gates_spread[:, P * c : P * (c + 1)], gate_columns[:, c : c + 1].to_broadcast([P, P]), identity[:])
+        gate_rows = keep.tile([P, S], F32, name="gate_rows")
+        nc.scalar.copy(out=gate_rows[:], in_=gates_spread[:])
 
         def half_list(h):
             return offsets[:, 16 * h : 16 * h + 16]
 
-        quads0 = keep.tile([P, S, 2], U32, name="quads0", align_bytes=64)
-        for u in range(2):
-            pairs = cast(u)
-            nc.vector.tensor_copy(quads0[:, :, u], pairs[:].indirect(offsets[:]))
+        sums = [[psum.tile([P, HALF], F32, name=f"sums{b}{h}") for h in range(2)] for b in range(BLOCKS)]
 
-        codes0, scales0 = [], []
-        picked1 = keep.tile([P, 2, S], U32, name="picked1", align_bytes=64)
-        for u in range(2):
-            pairs = cast(2 + u)
-            codes0.append(keep.tile([P, HALF], U32, name=f"codes0_{u}", tag=f"raw{2 + u}_0", align_bytes=64))
-            scales0.append(keep.tile([P, HALF], U8, name=f"scales0_{u}", tag=f"scales0_{u}", align_bytes=64))
-            nc.vector.quantize_mx(
-                out=codes0[u][:].bitcast(FP8X4), scales=scales0[u][:],
-                in_=quads0[:, HALF * u : HALF * (u + 1), :].rearrange("p s u -> p (s u)").bitcast(BF16),
-            )
-            for j0, j1 in ([(0, S)], LAST_PIECES)[u]:
-                nc.vector.tensor_copy(picked1[:, u, j0:j1], pairs[:].indirect(offsets[:, j0 // 16 : j1 // 16]))
-        quads1 = [keep.tile([P, HALF, 2], U32, name=f"quads1_{h}", tag=f"quads1_{h}", align_bytes=64) for h in range(2)]
-        for j0, j1 in LAST_PIECES:
-            h = j0 // HALF
-            nc.scalar.copy(
-                out=quads1[h][:, j0 - HALF * h : j1 - HALF * h, :], in_=picked1[:, :, j0:j1].rearrange("p u s -> p s u")
-            )
-        gates = keep.tile([P, S // P], F32, name="gates", tag="raw1_1", align_bytes=64)
-        nc.scalar.copy(out=gates[:], in_=gates_turned[:, 0 : S // P])
+        def gather_pair(i, first, flat):
+            for e in range(2):
+                plane = planes[2 * i + e]
+                nc.vector.tensor_copy(first[:, :, 2 * (i % 2) + e], plane[:].indirect(half_list(0)))
+                nc.scalar.activation(out=flat[:, e, :], in_=plane[:].indirect(half_list(1)), func=ACT.Copy)
+            return flat.rearrange("p e s -> p s e")
 
-        codes1 = [keep.tile([P, HALF], U32, name=f"codes1_{h}", tag=f"codes1_{h}", align_bytes=64) for h in range(2)]
-        scales1 = [keep.tile([P, HALF], U8, name=f"scales1_{h}", align_bytes=64) for h in range(2)]
+        def weave(dst, src):
+            nc.gpsimd.tensor_scalar(dst, src, 1.0, 0.0, ALU.mult, ALU.add)
 
-        def entries(j0, j1):
-            return offsets[:, j0 // 16 : j1 // 16]
-
-        old1 = [picked1[:, 0, HALF * h : HALF * (h + 1)].bitcast(F32) for h in range(2)]
-        for h in range(2):
-            nc.vector.quantize_mx(
-                out=codes1[h][:].bitcast(FP8X4), scales=scales1[h][:],
-                in_=quads1[h][:].rearrange("p s u -> p (s u)").bitcast(BF16),
-            )
-            nc.vector.tensor_copy(old1[h], windows[1][:].indirect(half_list(h)))
-        old0 = keep.tile([P, S], F32, name="old0", align_bytes=64)
-        nc.vector.tensor_copy(old0[:], windows[0][:].indirect(entries(0, S)))
-
-        def product(acc, z, c, b):
-            toks = slice(P * (c % 2), P * (c % 2 + 1))
-            codes, scales = [codes0, codes1][z][c // 2][:, toks], [scales0, scales1][z][c // 2][:, toks]
-            nc.tensor.matmul_mx(
-                out=acc, lhsT=codes.bitcast(FP8X4), lhsT_scale=scales,
-                rhs=w_words[z][:, 2 * P * b : 2 * P * (b + 1)].bitcast(FP4X4),
-                rhs_scale=w_scales[:, z * N + P * b : z * N + P * (b + 1)],
-                start=(z == 0), stop=(z == PASSES - 1),
-            )
-
-        def scatter(b, j0, j1, old, gated):
-            nc.vector.tensor_tensor(windows[b][:].indirect(entries(j0, j1)), old, gated, ALU.add)
-
-        def gate_on_scalar(sums, c0, b, bank, active_tag):
-            turned = psum.tile([P, 2, P], F32, name=f"turned{c0}{b}", tag=bank)
-            active = keep.tile([P, 2, P], F32, name=f"active{c0}{b}", tag=active_tag)
-            c = 0
-            for acc in sums:
-                nc.scalar.activation(out=active[:, c : c + acc.shape[1], :], in_=acc, func=ACT.Relu)
-                c = c + acc.shape[1]
-            for j in range(2):
-                scaled = keep.tile([P, P], F32, name=f"scaled{c0 + j}{b}")
-                nc.scalar.activation(
-                    out=scaled[:], in_=active[:, j, :], func=ACT.Copy, scale=gates[:, c0 + j : c0 + j + 1]
-                )
-                nc.tensor.transpose(turned[:, j, :], scaled[:], identity[:])
-            gated = keep.tile([P, HALF], F32, name=f"gated{c0}{b}")
-            nc.scalar.copy(out=gated[:], in_=turned[:].rearrange("p c t -> p (c t)"))
-            return gated
-
-        first = [psum.tile([P, P], F32, name=f"first{c}", tag=f"first{c}") for c in range(2)]
-        second = [psum.tile([P, 1, P], F32, name=f"second{c}") for c in range(2)]
-        for z in range(PASSES):
-            for c in range(2):
-                toks = slice(P * c, P * (c + 1))
+        def products(z, h, codes, scales):
+            for b in (1, 0):
                 nc.tensor.matmul_mx(
-                    out=first[c][:],
-                    lhsT=w_words[z][:, 2 * P : 4 * P].bitcast(FP4X4), lhsT_scale=w_scales[:, z * N + P : z * N + 2 * P],
-                    rhs=[codes0, codes1][z][0][:, toks].bitcast(FP8X4), rhs_scale=[scales0, scales1][z][0][:, toks],
+                    out=sums[b][h][:],
+                    lhsT=w_words[z][:, 2 * P * b : 2 * P * (b + 1)].bitcast(FP4X4),
+                    lhsT_scale=w_scales[:, z * N + P * b : z * N + P * (b + 1)],
+                    rhs=codes.bitcast(FP8X4), rhs_scale=scales,
                     start=(z == 0), stop=(z == PASSES - 1),
                 )
-            for c in range(2):
-                product(second[c][:, 0, :], z, c, 0)
-        gated_first = keep.tile([P, HALF], F32, name="gated_first", tag="quads1_1", align_bytes=64)
-        for c in range(2):
-            toks = slice(P * c, P * (c + 1))
-            active_first = keep.tile([P, P], F32, name=f"active_first{c}")
-            nc.scalar.activation(out=active_first[:], in_=first[c][:], func=ACT.Relu)
-            nc.gpsimd.tensor_tensor(gated_first[:, toks], active_first[:], gate_rows[:, toks], ALU.mult)
-        scatter(1, 0, HALF, old1[0], gated_first[:])
-        scatter(0, 0, HALF, old0[:, 0:HALF], gate_on_scalar([second[0][:], second[1][:]], 0, 0, "turned01", "active")[:])
 
-        def piece(c0, b, acc_bank, bank, active_tag):
-            acc = psum.tile([P, 2, P], F32, name=f"acc{c0}{b}", tag=acc_bank)
-            for c in range(2):
-                for z in range(PASSES):
-                    product(acc[:, c, :], z, c0 + c, b)
-            return gate_on_scalar([acc[:]], c0, b, bank, active_tag)
+        quads0 = keep.tile([P, S, PACK], BF16, name="quads0", tag="quads", align_bytes=64)
+        for i in range(2):
+            flat = keep.tile([P, 2, HALF], BF16, name=f"flat{i}", align_bytes=64)
+            weave(quads0[:, HALF:S, 2 * i : 2 * i + 2], gather_pair(i, quads0[:, 0:HALF, :], flat[:]))
+        codes0 = keep.tile([P, S], U32, name="codes0", align_bytes=64)
+        scales0 = keep.tile([P, S], U8, name="scales0", align_bytes=64)
+        nc.vector.quantize_mx(out=codes0[:].bitcast(FP8X4), scales=scales0[:], in_=quads0[:].rearrange("p s t -> p (s t)"))
+        for h in range(2):
+            products(0, h, codes0[:, HALF * h : HALF * (h + 1)], scales0[:, HALF * h : HALF * (h + 1)])
 
-        scatter(1, HALF, S, old1[1], piece(2, 1, "first0", "turned21", "active")[:])
+        quads1 = [
+            keep.tile([P, HALF, PACK], BF16, name="quads10", align_bytes=64),
+            keep.tile([P, HALF, PACK], BF16, name="quads11", tag="quads", align_bytes=64),
+        ]
+        flat1 = keep.tile([P, 3, HALF], BF16, name="flat_pass1", align_bytes=64)
+        weave(quads1[1][:, :, 0:2], gather_pair(2, quads1[0][:], flat1[:, 1:3, :]))
+        nc.vector.tensor_copy(quads1[1][:, :, 2:4], gather_pair(3, quads1[0][:], flat1[:, 0:2, :]))
+        for h in range(2):
+            codes = keep.tile([P, HALF], U32, name=f"codes1{h}", align_bytes=64)
+            scales = keep.tile([P, HALF], U8, name=f"scales1{h}", align_bytes=64)
+            nc.vector.quantize_mx(
+                out=codes[:].bitcast(FP8X4), scales=scales[:], in_=quads1[h][:].rearrange("p s t -> p (s t)")
+            )
+            products(1, h, codes[:], scales[:])
+
+        old = [keep.tile([P, S], F32, name=f"old{b}") for b in range(BLOCKS)]
+        gated1 = [keep.tile([P, HALF], F32, name=f"gated1{h}", tag=f"gated{h}") for h in range(2)]
+        new = [keep.tile([P, HALF], F32, name=f"new{h}") for h in range(2)]
+
+        def half(h):
+            return slice(HALF * h, HALF * (h + 1))
+
+        def gating(dst, b, h):
+            nc.vector.scalar_tensor_tensor(
+                out=dst[:], in0=sums[b][h][:], scalar=0.0, in1=gate_rows[:, half(h)], op0=ALU.max, op1=ALU.mult
+            )
+
+        for h in range(2):
+            nc.scalar.activation(out=old[1][:, half(h)], in_=windows[1][:].indirect(half_list(h)), func=ACT.Copy)
+        gated00 = keep.tile([P, HALF], F32, name="gated00")
+        gating(gated1[0], 1, 0)
+        gating(gated00, 0, 0)
+        gating(gated1[1], 1, 1)
+        for h in range(2):
+            nc.gpsimd.tensor_tensor(new[h][:], old[1][:, half(h)], gated1[h][:], ALU.add)
+        nc.vector.tensor_copy(old[0][:], windows[0][:].indirect(offsets[:]))
+        gated01 = keep.tile([P, HALF], F32, name="gated01", tag="gated1")
+        gating(gated01, 0, 1)
+        gated0 = [gated00, gated01]
+        for h in range(2):
+            nc.scalar.activation(out=windows[1][:].indirect(half_list(h)), in_=new[h][:], func=ACT.Copy)
+            nc.vector.tensor_tensor(windows[0][:].indirect(half_list(h)), old[0][:, half(h)], gated0[h][:], ALU.add)
         nc.sync.dma_start(out=out[P : 2 * P, :], in_=windows[1][:])
-        scatter(0, HALF, S, old0[:, HALF:S], piece(2, 0, "first1", "turned20", "active")[:])
         nc.sync.dma_start(out=out[0:P, :], in_=windows[0][:])

@@ -35,9 +35,6 @@ def tile_picked_modres_linrelu_l_kernel(tc, xT, gate, res, w1_words, w1_scales, 
 
         w_scales = keep.tile([P, PASSES * N], U8, name="w_scales", align_bytes=64)
         nc.gpsimd.memset(w_scales[:].bitcast(I32), 0)
-        warm = keep.tile([P, 8], F32, name="warm")
-        nc.vector.memset(warm[:, 0:1], 0.0)
-        nc.scalar.activation(out=warm[:, 4:5], in_=warm[:, 0:1], func=ACT.Copy)
         gate_chunks = keep.tile([P, P], F32, name="gate_chunks")
         nc.gpsimd.memset(gate_chunks[:], 0.0)
         nc.scalar.dma_start(out=gate_chunks[0 : S // P, :], in_=gate[0, :].rearrange("(c p) -> c p", p=P))

@@ -41,13 +41,14 @@ def tile_picked_modres_linrelu_l_kernel(tc, xT, gate, res, w1_words, w1_scales, 
         identity = keep.tile([P, P], F32, name="identity")
         make_identity(nc, identity[:])
         for q in range(4):
-            queue = nc.scalar if q < 2 else nc.gpsimd
+            queue = nc.scalar if q == 0 else nc.gpsimd
             queue.dma_start(
                 out=w_scales[32 * q : 32 * q + 4, :].rearrange("r (z c) -> r z c", z=PASSES).bitcast(I32),
                 in_=w1_scales[:, 4 * q : 4 * q + 4, :].rearrange("z r c -> r z c").bitcast(I32),
             )
 
-        w_words = [keep.tile([P, 2 * N], U8, name=f"w_words{z}", align_bytes=64) for z in range(PASSES)]
+        w_both = keep.tile([P, PASSES * 2 * N], U8, name="w_both", align_bytes=64)
+        w_words = [w_both[:, 2 * N * z : 2 * N * (z + 1)] for z in range(PASSES)]
         planes = []
         for i in range(PASSES * PACK):
             plane = keep.tile([P, T], F32, name=f"plane{i}")
@@ -56,11 +57,13 @@ def tile_picked_modres_linrelu_l_kernel(tc, xT, gate, res, w1_words, w1_scales, 
             if i == 0:
                 nc.sync.dma_start(offsets[:], offs)
             if i == 5:
-                nc.sync.dma_start(out=w_words[0][:].bitcast(I32), in_=w1_words[0].bitcast(I32))
+                nc.sync.dma_start(
+                    out=w_both[:].rearrange("p (z c) -> p z c", z=PASSES).bitcast(I32),
+                    in_=w1_words.rearrange("z p c -> p z c").bitcast(I32),
+                )
 
         windows = [keep.tile([P, T], F32, name=f"res{b}") for b in range(BLOCKS)]
         nc.sync.dma_start(out=windows[1][:], in_=res[P : 2 * P, :])
-        nc.sync.dma_start(out=w_words[1][:].bitcast(I32), in_=w1_words[1].bitcast(I32))
         nc.sync.dma_start(out=windows[0][:], in_=res[0:P, :])
 
         gates_turned = psum.tile([P, P], F32, name="gates_turned")
@@ -73,82 +76,83 @@ def tile_picked_modres_linrelu_l_kernel(tc, xT, gate, res, w1_words, w1_scales, 
         gate_rows = keep.tile([P, S], F32, name="gate_rows")
         nc.scalar.copy(out=gate_rows[:], in_=gates_spread[:])
 
-        def half_list(h):
-            return offsets[:, 16 * h : 16 * h + 16]
+        def entries(j0, j1):
+            return offsets[:, j0 // 16 : j1 // 16]
 
-        sums = [[psum.tile([P, HALF], F32, name=f"sums{b}{h}") for h in range(2)] for b in range(BLOCKS)]
+        pieces = [[(0, HALF), (HALF, S)], [(0, P), (P, HALF), (HALF, S)]]
+        sums = {(b, j0): psum.tile([P, j1 - j0], F32, name=f"sums{b}_{j0}") for b in range(BLOCKS) for j0, j1 in pieces[b]}
 
-        def gather_pair(i, first, flat):
+        def gather_pair(i, first, flat, last_cuts):
             for e in range(2):
                 plane = planes[2 * i + e]
-                nc.vector.tensor_copy(first[:, :, 2 * (i % 2) + e], plane[:].indirect(half_list(0)))
-                nc.scalar.activation(out=flat[:, e, :], in_=plane[:].indirect(half_list(1)), func=ACT.Copy)
+                for j0, j1 in ([(0, HALF)], last_cuts)[e]:
+                    nc.vector.tensor_copy(first[:, j0:j1, 2 * (i % 2) + e], plane[:].indirect(entries(j0, j1)))
+                nc.scalar.activation(out=flat[:, e, :], in_=plane[:].indirect(entries(HALF, S)), func=ACT.Copy)
             return flat.rearrange("p e s -> p s e")
 
         def weave(dst, src):
             nc.gpsimd.tensor_scalar(dst, src, 1.0, 0.0, ALU.mult, ALU.add)
 
-        def products(z, h, codes, scales):
-            for b in (1, 0):
-                nc.tensor.matmul_mx(
-                    out=sums[b][h][:],
-                    lhsT=w_words[z][:, 2 * P * b : 2 * P * (b + 1)].bitcast(FP4X4),
-                    lhsT_scale=w_scales[:, z * N + P * b : z * N + P * (b + 1)],
-                    rhs=codes.bitcast(FP8X4), rhs_scale=scales,
-                    start=(z == 0), stop=(z == PASSES - 1),
-                )
+        codes = [keep.tile([P, S], U32, name=f"codes{z}", align_bytes=64) for z in range(PASSES)]
+        scales = [keep.tile([P, S], U8, name=f"scales{z}", align_bytes=64) for z in range(PASSES)]
+
+        def quantise(z, j0, j1, quads):
+            nc.vector.quantize_mx(
+                out=codes[z][:, j0:j1].bitcast(FP8X4), scales=scales[z][:, j0:j1], in_=quads.rearrange("p s t -> p (s t)")
+            )
+
+        def product(z, b, j0, j1):
+            nc.tensor.matmul_mx(
+                out=sums[b, j0][:],
+                lhsT=w_words[z][:, 2 * P * b : 2 * P * (b + 1)].bitcast(FP4X4),
+                lhsT_scale=w_scales[:, z * N + P * b : z * N + P * (b + 1)],
+                rhs=codes[z][:, j0:j1].bitcast(FP8X4), rhs_scale=scales[z][:, j0:j1],
+                start=(z == 0), stop=(z == PASSES - 1),
+            )
+
+        order = [(1, 0, P), (1, P, HALF), (0, 0, HALF), (1, HALF, S), (0, HALF, S)]
 
         quads0 = keep.tile([P, S, PACK], BF16, name="quads0", tag="quads", align_bytes=64)
         for i in range(2):
             flat = keep.tile([P, 2, HALF], BF16, name=f"flat{i}", align_bytes=64)
-            weave(quads0[:, HALF:S, 2 * i : 2 * i + 2], gather_pair(i, quads0[:, 0:HALF, :], flat[:]))
-        codes0 = keep.tile([P, S], U32, name="codes0", align_bytes=64)
-        scales0 = keep.tile([P, S], U8, name="scales0", align_bytes=64)
-        nc.vector.quantize_mx(out=codes0[:].bitcast(FP8X4), scales=scales0[:], in_=quads0[:].rearrange("p s t -> p (s t)"))
-        for h in range(2):
-            products(0, h, codes0[:, HALF * h : HALF * (h + 1)], scales0[:, HALF * h : HALF * (h + 1)])
+            weave(quads0[:, HALF:S, 2 * i : 2 * i + 2], gather_pair(i, quads0[:, 0:HALF, :], flat[:], [(0, HALF)]))
+        quantise(0, 0, S, quads0[:])
+        for b, j0, j1 in order:
+            product(0, b, j0, j1)
 
-        quads1 = [
-            keep.tile([P, HALF, PACK], BF16, name="quads10", align_bytes=64),
-            keep.tile([P, HALF, PACK], BF16, name="quads11", tag="quads", align_bytes=64),
-        ]
+        quads10 = keep.tile([P, HALF, PACK], BF16, name="quads10", align_bytes=64)
+        quads11 = keep.tile([P, HALF, PACK], BF16, name="quads11", tag="quads", align_bytes=64)
         flat1 = keep.tile([P, 3, HALF], BF16, name="flat_pass1", align_bytes=64)
-        weave(quads1[1][:, :, 0:2], gather_pair(2, quads1[0][:], flat1[:, 1:3, :]))
-        nc.vector.tensor_copy(quads1[1][:, :, 2:4], gather_pair(3, quads1[0][:], flat1[:, 0:2, :]))
-        for h in range(2):
-            codes = keep.tile([P, HALF], U32, name=f"codes1{h}", align_bytes=64)
-            scales = keep.tile([P, HALF], U8, name=f"scales1{h}", align_bytes=64)
-            nc.vector.quantize_mx(
-                out=codes[:].bitcast(FP8X4), scales=scales[:], in_=quads1[h][:].rearrange("p s t -> p (s t)")
-            )
-            products(1, h, codes[:], scales[:])
+        weave(quads11[:, :, 0:2], gather_pair(2, quads10[:], flat1[:, 1:3, :], [(0, HALF)]))
+        last_pair = gather_pair(3, quads10[:], flat1[:, 0:2, :], [(0, P), (P, HALF)])
+        quantise(1, 0, P, quads10[:, 0:P, :])
+        nc.vector.tensor_copy(quads11[:, :, 2:4], last_pair)
+        quantise(1, P, HALF, quads10[:, P:HALF, :])
+        quantise(1, HALF, S, quads11[:])
+        for b, j0, j1 in order:
+            product(1, b, j0, j1)
 
-        old = [keep.tile([P, S], F32, name=f"old{b}") for b in range(BLOCKS)]
-        gated1 = [keep.tile([P, HALF], F32, name=f"gated1{h}", tag=f"gated{h}") for h in range(2)]
-        new = [keep.tile([P, HALF], F32, name=f"new{h}") for h in range(2)]
+        old1 = keep.tile([P, S], F32, name="old1")
+        old0 = keep.tile([P, S], F32, name="old0")
+        gated = [keep.tile([P, S], F32, name=f"gated{b}") for b in range(BLOCKS)]
+        new1 = keep.tile([P, S], F32, name="new1")
 
-        def half(h):
-            return slice(HALF * h, HALF * (h + 1))
-
-        def gating(dst, b, h):
+        def gating(b, j0, j1):
             nc.vector.scalar_tensor_tensor(
-                out=dst[:], in0=sums[b][h][:], scalar=0.0, in1=gate_rows[:, half(h)], op0=ALU.max, op1=ALU.mult
+                out=gated[b][:, j0:j1], in0=sums[b, j0][:], scalar=0.0, in1=gate_rows[:, j0:j1], op0=ALU.max, op1=ALU.mult
             )
 
-        for h in range(2):
-            nc.scalar.activation(out=old[1][:, half(h)], in_=windows[1][:].indirect(half_list(h)), func=ACT.Copy)
-        gated00 = keep.tile([P, HALF], F32, name="gated00")
-        gating(gated1[0], 1, 0)
-        gating(gated00, 0, 0)
-        gating(gated1[1], 1, 1)
-        for h in range(2):
-            nc.gpsimd.tensor_tensor(new[h][:], old[1][:, half(h)], gated1[h][:], ALU.add)
-        nc.vector.tensor_copy(old[0][:], windows[0][:].indirect(offsets[:]))
-        gated01 = keep.tile([P, HALF], F32, name="gated01", tag="gated1")
-        gating(gated01, 0, 1)
-        gated0 = [gated00, gated01]
-        for h in range(2):
-            nc.scalar.activation(out=windows[1][:].indirect(half_list(h)), in_=new[h][:], func=ACT.Copy)
-            nc.vector.tensor_tensor(windows[0][:].indirect(half_list(h)), old[0][:, half(h)], gated0[h][:], ALU.add)
+        for j0, j1 in pieces[0]:
+            nc.scalar.activation(out=old1[:, j0:j1], in_=windows[1][:].indirect(entries(j0, j1)), func=ACT.Copy)
+        for b, j0, j1 in order[:4]:
+            gating(b, j0, j1)
+        for j0, j1 in pieces[1]:
+            nc.gpsimd.tensor_tensor(new1[:, j0:j1], old1[:, j0:j1], gated[1][:, j0:j1], ALU.add)
+        nc.vector.tensor_copy(old0[:, P:S], windows[0][:].indirect(entries(P, S)))
+        gating(0, HALF, S)
+        nc.scalar.activation(out=windows[1][:].indirect(entries(0, P)), in_=new1[:, 0:P], func=ACT.Copy)
+        nc.scalar.activation(out=old0[:, 0:P], in_=windows[0][:].indirect(entries(0, P)), func=ACT.Copy)
+        nc.scalar.activation(out=windows[1][:].indirect(entries(P, S)), in_=new1[:, P:S], func=ACT.Copy)
+        nc.vector.tensor_tensor(windows[0][:].indirect(offsets[:]), old0[:], gated[0][:], ALU.add)
         nc.sync.dma_start(out=out[P : 2 * P, :], in_=windows[1][:])
         nc.sync.dma_start(out=out[0:P, :], in_=windows[0][:])

@@ -1,7 +1,6 @@
 from contextlib import ExitStack
 
 import concourse.mybir as mybir
-from concourse.masks import make_identity
 
 K, T, S, N = 1024, 1024, 512, 256
 FLOPS = 2 * K * S * N
@@ -35,11 +34,6 @@ def tile_picked_modres_linrelu_l_kernel(tc, xT, gate, res, w1_words, w1_scales, 
 
         w_scales = keep.tile([P, PASSES * N], U8, name="w_scales", align_bytes=64)
         nc.gpsimd.memset(w_scales[:].bitcast(I32), 0)
-        gate_chunks = keep.tile([P, P], F32, name="gate_chunks")
-        nc.gpsimd.memset(gate_chunks[:], 0.0)
-        nc.scalar.dma_start(out=gate_chunks[0 : S // P, :], in_=gate[0, :].rearrange("(c p) -> c p", p=P))
-        identity = keep.tile([P, P], F32, name="identity")
-        make_identity(nc, identity[:])
         for q in range(4):
             queue = nc.scalar if q == 0 else nc.gpsimd
             queue.dma_start(
@@ -64,17 +58,9 @@ def tile_picked_modres_linrelu_l_kernel(tc, xT, gate, res, w1_words, w1_scales, 
 
         windows = [keep.tile([P, T], F32, name=f"res{b}") for b in range(BLOCKS)]
         nc.sync.dma_start(out=windows[1][:], in_=res[P : 2 * P, :])
-        nc.sync.dma_start(out=windows[0][:], in_=res[0:P, :])
-
-        gates_turned = psum.tile([P, P], F32, name="gates_turned")
-        nc.tensor.transpose(gates_turned[:], gate_chunks[:], identity[:])
-        gate_columns = keep.tile([P, S // P], F32, name="gate_columns")
-        nc.scalar.copy(out=gate_columns[:], in_=gates_turned[:, 0 : S // P])
-        gates_spread = psum.tile([P, S], F32, name="gates_spread")
-        for c in range(S // P):
-            nc.tensor.transpose(gates_spread[:, P * c : P * (c + 1)], gate_columns[:, c : c + 1].to_broadcast([P, P]), identity[:])
         gate_rows = keep.tile([P, S], F32, name="gate_rows")
-        nc.scalar.copy(out=gate_rows[:], in_=gates_spread[:])
+        nc.sync.dma_start(out=gate_rows[:], in_=gate)
+        nc.sync.dma_start(out=windows[0][:], in_=res[0:P, :])
 
         def entries(j0, j1):
             return offsets[:, j0 // 16 : j1 // 16]
@@ -87,7 +73,10 @@ def tile_picked_modres_linrelu_l_kernel(tc, xT, gate, res, w1_words, w1_scales, 
                 plane = planes[2 * i + e]
                 for j0, j1 in ([(0, HALF)], last_cuts)[e]:
                     nc.vector.tensor_copy(first[:, j0:j1, 2 * (i % 2) + e], plane[:].indirect(entries(j0, j1)))
-                nc.scalar.activation(out=flat[:, e, :], in_=plane[:].indirect(entries(HALF, S)), func=ACT.Copy)
+                for j0, j1 in ([(0, HALF)], last_cuts)[e]:
+                    nc.scalar.activation(
+                        out=flat[:, e, j0:j1], in_=plane[:].indirect(entries(HALF + j0, HALF + j1)), func=ACT.Copy
+                    )
             return flat.rearrange("p e s -> p s e")
 
         def weave(dst, src):
@@ -112,7 +101,7 @@ def tile_picked_modres_linrelu_l_kernel(tc, xT, gate, res, w1_words, w1_scales, 
 
         order = [(1, 0, P), (1, P, HALF), (0, 0, HALF), (1, HALF, S), (0, HALF, S)]
 
-        quads0 = keep.tile([P, S, PACK], BF16, name="quads0", tag="quads", align_bytes=64)
+        quads0 = keep.tile([P, S, PACK], BF16, name="quads0", align_bytes=64)
         for i in range(2):
             flat = keep.tile([P, 2, HALF], BF16, name=f"flat{i}", align_bytes=64)
             weave(quads0[:, HALF:S, 2 * i : 2 * i + 2], gather_pair(i, quads0[:, 0:HALF, :], flat[:], [(0, HALF)]))
@@ -121,14 +110,17 @@ def tile_picked_modres_linrelu_l_kernel(tc, xT, gate, res, w1_words, w1_scales, 
             product(0, b, j0, j1)
 
         quads10 = keep.tile([P, HALF, PACK], BF16, name="quads10", align_bytes=64)
-        quads11 = keep.tile([P, HALF, PACK], BF16, name="quads11", tag="quads", align_bytes=64)
-        flat1 = keep.tile([P, 3, HALF], BF16, name="flat_pass1", align_bytes=64)
-        weave(quads11[:, :, 0:2], gather_pair(2, quads10[:], flat1[:, 1:3, :], [(0, HALF)]))
-        last_pair = gather_pair(3, quads10[:], flat1[:, 0:2, :], [(0, P), (P, HALF)])
+        quads11 = keep.tile([P, HALF, PACK], BF16, name="quads11", align_bytes=64)
+        flat2 = keep.tile([P, 2, HALF], BF16, name="flat2", align_bytes=64)
+        nc.scalar.copy(out=quads11[:, :, 0:2], in_=gather_pair(2, quads10[:], flat2[:], [(0, HALF)]))
+        flat3 = keep.tile([P, 2, HALF], BF16, name="flat3", align_bytes=64)
+        last_pair = gather_pair(3, quads10[:], flat3[:], [(0, P), (P, HALF)])
         quantise(1, 0, P, quads10[:, 0:P, :])
-        nc.vector.tensor_copy(quads11[:, :, 2:4], last_pair)
+        nc.scalar.copy(out=quads11[:, 0:P, 2:4], in_=last_pair[:, 0:P, :])
+        nc.vector.tensor_copy(quads11[:, P:HALF, 2:4], last_pair[:, P:HALF, :])
         quantise(1, P, HALF, quads10[:, P:HALF, :])
-        quantise(1, HALF, S, quads11[:])
+        quantise(1, HALF, HALF + P, quads11[:, 0:P, :])
+        quantise(1, HALF + P, S, quads11[:, P:HALF, :])
         for b, j0, j1 in order:
             product(1, b, j0, j1)
 

@@ -35,8 +35,7 @@ def tile_picked_modres_linrelu_l_kernel(tc, xT, gate, res, w1_words, w1_scales, 
         w_scales = keep.tile([P, PASSES * N], U8, name="w_scales", align_bytes=64)
         nc.gpsimd.memset(w_scales[:].bitcast(I32), 0)
         for q in range(4):
-            queue = nc.scalar if q == 0 else nc.gpsimd
-            queue.dma_start(
+            nc.scalar.dma_start(
                 out=w_scales[32 * q : 32 * q + 4, :].rearrange("r (z c) -> r z c", z=PASSES).bitcast(I32),
                 in_=w1_scales[:, 4 * q : 4 * q + 4, :].rearrange("z r c -> r z c").bitcast(I32),
             )

@@ -21,6 +21,7 @@ PACK = 4
 PASSES = 2
 BLOCKS = 2
 HALF = S // 2
+SHARE = 192
 
 
 def tile_picked_modres_linrelu_l_kernel(tc, xT, gate, res, w1_words, w1_scales, offs, out):
@@ -64,7 +65,7 @@ def tile_picked_modres_linrelu_l_kernel(tc, xT, gate, res, w1_words, w1_scales, 
         def entries(j0, j1):
             return offsets[:, j0 // 16 : j1 // 16]
 
-        pieces = [[(0, HALF), (HALF, S)], [(0, P), (P, HALF), (HALF, S)]]
+        pieces = [[(0, P), (P, HALF), (HALF, S)], [(0, P), (P, HALF), (HALF, S)]]
         sums = {(b, j0): psum.tile([P, j1 - j0], F32, name=f"sums{b}_{j0}") for b in range(BLOCKS) for j0, j1 in pieces[b]}
 
         def gather_pair(i, first, flat, last_cuts):
@@ -98,7 +99,7 @@ def tile_picked_modres_linrelu_l_kernel(tc, xT, gate, res, w1_words, w1_scales, 
                 start=(z == 0), stop=(z == PASSES - 1),
             )
 
-        order = [(1, 0, P), (1, P, HALF), (0, 0, HALF), (1, HALF, S), (0, HALF, S)]
+        order = [(b, j0, j1) for j0, j1 in pieces[1] for b in (1, 0)]
 
         quads0 = keep.tile([P, S, PACK], BF16, name="quads0", align_bytes=64)
         for i in range(2):
@@ -133,16 +134,16 @@ def tile_picked_modres_linrelu_l_kernel(tc, xT, gate, res, w1_words, w1_scales, 
                 out=gated[b][:, j0:j1], in0=sums[b, j0][:], scalar=0.0, in1=gate_rows[:, j0:j1], op0=ALU.max, op1=ALU.mult
             )
 
-        for j0, j1 in pieces[0]:
+        for j0, j1 in [(0, HALF), (HALF, S)]:
             nc.scalar.activation(out=old1[:, j0:j1], in_=windows[1][:].indirect(entries(j0, j1)), func=ACT.Copy)
-        for b, j0, j1 in order[:4]:
+        for b, j0, j1 in order[:5]:
             gating(b, j0, j1)
         for j0, j1 in pieces[1]:
             nc.gpsimd.tensor_tensor(new1[:, j0:j1], old1[:, j0:j1], gated[1][:, j0:j1], ALU.add)
-        nc.vector.tensor_copy(old0[:, P:S], windows[0][:].indirect(entries(P, S)))
+        nc.vector.tensor_copy(old0[:, SHARE:S], windows[0][:].indirect(entries(SHARE, S)))
         gating(0, HALF, S)
         nc.scalar.activation(out=windows[1][:].indirect(entries(0, P)), in_=new1[:, 0:P], func=ACT.Copy)
-        nc.scalar.activation(out=old0[:, 0:P], in_=windows[0][:].indirect(entries(0, P)), func=ACT.Copy)
+        nc.scalar.activation(out=old0[:, 0:SHARE], in_=windows[0][:].indirect(entries(0, SHARE)), func=ACT.Copy)
         nc.scalar.activation(out=windows[1][:].indirect(entries(P, S)), in_=new1[:, P:S], func=ACT.Copy)
         nc.vector.tensor_tensor(windows[0][:].indirect(offsets[:]), old0[:], gated[0][:], ALU.add)
         nc.sync.dma_start(out=out[P : 2 * P, :], in_=windows[1][:])

from contextlib import ExitStack

import concourse.mybir as mybir

K, T, S, N = 1024, 1024, 512, 256
FLOPS = 2 * K * S * N

F32 = mybir.dt.float32
BF16 = mybir.dt.bfloat16
U32 = mybir.dt.uint32
I32 = mybir.dt.int32
U16 = mybir.dt.uint16
U8 = mybir.dt.uint8
FP8X4 = mybir.dt.float8_e4m3fn_x4
FP4X4 = mybir.dt.float4_e2m1fn_x4
ALU = mybir.AluOpType
ACT = mybir.ActivationFunctionType

P = 128
PACK = 4
PASSES = 2
BLOCKS = 2
HALF = S // 2
SHARE = 192


def tile_picked_modres_linrelu_l_kernel(tc, xT, gate, res, w1_words, w1_scales, offs, out):
    nc = tc.nc
    with ExitStack() as ctx:
        keep = ctx.enter_context(tc.tile_pool(name="keep", bufs=1))
        psum = ctx.enter_context(tc.psum_pool(name="psum", bufs=1))

        offsets = keep.tile([P, S // 16], U16, name="offsets")
        x_rows = xT.rearrange("(z p t) c -> z t p c", z=PASSES, p=P, t=PACK)

        w_scales = keep.tile([P, PASSES * N], U8, name="w_scales", align_bytes=64)
        nc.gpsimd.memset(w_scales[:].bitcast(I32), 0)
        for q in range(4):
            nc.scalar.dma_start(
                out=w_scales[32 * q : 32 * q + 4, :].rearrange("r (z c) -> r z c", z=PASSES).bitcast(I32),
                in_=w1_scales[:, 4 * q : 4 * q + 4, :].rearrange("z r c -> r z c").bitcast(I32),
            )

        w_both = keep.tile([P, PASSES * 2 * N], U8, name="w_both", align_bytes=64)
        w_words = [w_both[:, 2 * N * z : 2 * N * (z + 1)] for z in range(PASSES)]
        planes = []
        for i in range(PASSES * PACK):
            plane = keep.tile([P, T], F32, name=f"plane{i}")
            nc.sync.dma_start(out=plane[:], in_=x_rows[i // PACK, i % PACK])
            planes.append(plane)
            if i == 0:
                nc.sync.dma_start(offsets[:], offs)
            if i == 5:
                nc.sync.dma_start(
                    out=w_both[:].rearrange("p (z c) -> p z c", z=PASSES).bitcast(I32),
                    in_=w1_words.rearrange("z p c -> p z c").bitcast(I32),
                )

        windows = [keep.tile([P, T], F32, name=f"res{b}") for b in range(BLOCKS)]
        nc.sync.dma_start(out=windows[1][:], in_=res[P : 2 * P, :])
        gate_rows = keep.tile([P, S], F32, name="gate_rows")
        nc.sync.dma_start(out=gate_rows[:], in_=gate)
        nc.sync.dma_start(out=windows[0][:], in_=res[0:P, :])

        def entries(j0, j1):
            return offsets[:, j0 // 16 : j1 // 16]

        pieces = [[(0, P), (P, HALF), (HALF, S)], [(0, P), (P, HALF), (HALF, S)]]
        sums = {(b, j0): psum.tile([P, j1 - j0], F32, name=f"sums{b}_{j0}") for b in range(BLOCKS) for j0, j1 in pieces[b]}

        def gather_pair(i, first, flat, last_cuts):
            for e in range(2):
                plane = planes[2 * i + e]
                for j0, j1 in ([(0, HALF)], last_cuts)[e]:
                    nc.vector.tensor_copy(first[:, j0:j1, 2 * (i % 2) + e], plane[:].indirect(entries(j0, j1)))
                for j0, j1 in ([(0, HALF)], last_cuts)[e]:
                    nc.scalar.activation(
                        out=flat[:, e, j0:j1], in_=plane[:].indirect(entries(HALF + j0, HALF + j1)), func=ACT.Copy
                    )
            return flat.rearrange("p e s -> p s e")

        def weave(dst, src):
            nc.gpsimd.tensor_scalar(dst, src, 1.0, 0.0, ALU.mult, ALU.add)

        codes = [keep.tile([P, S], U32, name=f"codes{z}", align_bytes=64) for z in range(PASSES)]
        scales = [keep.tile([P, S], U8, name=f"scales{z}", align_bytes=64) for z in range(PASSES)]

        def quantise(z, j0, j1, quads):
            nc.vector.quantize_mx(
                out=codes[z][:, j0:j1].bitcast(FP8X4), scales=scales[z][:, j0:j1], in_=quads.rearrange("p s t -> p (s t)")
            )

        def product(z, b, j0, j1):
            nc.tensor.matmul_mx(
                out=sums[b, j0][:],
                lhsT=w_words[z][:, 2 * P * b : 2 * P * (b + 1)].bitcast(FP4X4),
                lhsT_scale=w_scales[:, z * N + P * b : z * N + P * (b + 1)],
                rhs=codes[z][:, j0:j1].bitcast(FP8X4), rhs_scale=scales[z][:, j0:j1],
                start=(z == 0), stop=(z == PASSES - 1),
            )

        order = [(b, j0, j1) for j0, j1 in pieces[1] for b in (1, 0)]

        quads0 = keep.tile([P, S, PACK], BF16, name="quads0", align_bytes=64)
        for i in range(2):
            flat = keep.tile([P, 2, HALF], BF16, name=f"flat{i}", align_bytes=64)
            weave(quads0[:, HALF:S, 2 * i : 2 * i + 2], gather_pair(i, quads0[:, 0:HALF, :], flat[:], [(0, HALF)]))
        quantise(0, 0, S, quads0[:])
        for b, j0, j1 in order:
            product(0, b, j0, j1)

        quads10 = keep.tile([P, HALF, PACK], BF16, name="quads10", align_bytes=64)
        quads11 = keep.tile([P, HALF, PACK], BF16, name="quads11", align_bytes=64)
        flat2 = keep.tile([P, 2, HALF], BF16, name="flat2", align_bytes=64)
        nc.scalar.copy(out=quads11[:, :, 0:2], in_=gather_pair(2, quads10[:], flat2[:], [(0, HALF)]))
        flat3 = keep.tile([P, 2, HALF], BF16, name="flat3", align_bytes=64)
        last_pair = gather_pair(3, quads10[:], flat3[:], [(0, P), (P, HALF)])
        quantise(1, 0, P, quads10[:, 0:P, :])
        nc.scalar.copy(out=quads11[:, 0:P, 2:4], in_=last_pair[:, 0:P, :])
        nc.vector.tensor_copy(quads11[:, P:HALF, 2:4], last_pair[:, P:HALF, :])
        quantise(1, P, HALF, quads10[:, P:HALF, :])
        quantise(1, HALF, HALF + P, quads11[:, 0:P, :])
        quantise(1, HALF + P, S, quads11[:, P:HALF, :])
        for b, j0, j1 in order:
            product(1, b, j0, j1)

        old1 = keep.tile([P, S], F32, name="old1")
        old0 = keep.tile([P, S], F32, name="old0")
        gated = [keep.tile([P, S], F32, name=f"gated{b}") for b in range(BLOCKS)]
        new1 = keep.tile([P, S], F32, name="new1")

        def gating(b, j0, j1):
            nc.vector.scalar_tensor_tensor(
                out=gated[b][:, j0:j1], in0=sums[b, j0][:], scalar=0.0, in1=gate_rows[:, j0:j1], op0=ALU.max, op1=ALU.mult
            )

        for j0, j1 in [(0, HALF), (HALF, S)]:
            nc.scalar.activation(out=old1[:, j0:j1], in_=windows[1][:].indirect(entries(j0, j1)), func=ACT.Copy)
        for b, j0, j1 in order[:5]:
            gating(b, j0, j1)
        for j0, j1 in pieces[1]:
            nc.gpsimd.tensor_tensor(new1[:, j0:j1], old1[:, j0:j1], gated[1][:, j0:j1], ALU.add)
        nc.vector.tensor_copy(old0[:, SHARE:S], windows[0][:].indirect(entries(SHARE, S)))
        gating(0, HALF, S)
        nc.scalar.activation(out=windows[1][:].indirect(entries(0, P)), in_=new1[:, 0:P], func=ACT.Copy)
        nc.scalar.activation(out=old0[:, 0:SHARE], in_=windows[0][:].indirect(entries(0, SHARE)), func=ACT.Copy)
        nc.scalar.activation(out=windows[1][:].indirect(entries(P, S)), in_=new1[:, P:S], func=ACT.Copy)
        nc.vector.tensor_tensor(windows[0][:].indirect(offsets[:]), old0[:], gated[0][:], ALU.add)
        nc.sync.dma_start(out=out[P : 2 * P, :], in_=windows[1][:])
        nc.sync.dma_start(out=out[0:P, :], in_=windows[0][:])
